import numpy as np
import ml_dtypes


def mxq(x, axis, fmt="e4m3"):
    dtype, down = {"e4m3": (ml_dtypes.float8_e4m3fn, 7), "e5m2": (ml_dtypes.float8_e5m2, 14)}[fmt]
    v = np.moveaxis(np.asarray(x, np.float32).astype(ml_dtypes.bfloat16).astype(np.float64), axis, -1)
    blocks = v.reshape(v.shape[:-1] + (-1, 32))
    amax = np.abs(blocks).max(-1, keepdims=True)
    byte = np.maximum(np.where(amax > 0, np.frexp(amax)[1] - 1 + 127, 0) - down, 1)
    scale = np.exp2(byte - 127.0)
    codes = (blocks / scale).astype(np.float32).astype(dtype).astype(np.float64)
    return np.moveaxis((codes * scale).reshape(v.shape), -1, axis)


WIDE = False


def mx_kscale(k):
    if not WIDE:
        return np.ones(k)
    levels = np.array([10, -10, 5, -5, 0])
    if k % 512:
        return np.exp2(np.random.permutation(np.resize(levels, k // 32))).repeat(32)
    a = np.empty((k // 512, 16))
    for p in range(k // 512):
        a[p, :8] = np.random.permutation(np.resize(levels, 8))
        for g in range(8):
            far = levels[np.abs(levels - a[p, g]) >= 10]
            a[p, g + 8] = far[np.random.randint(len(far))]
    return np.exp2(a.ravel()).repeat(32)


def f64(x):
    return np.asarray(x).astype(np.float64)


def striped8(idx):
    return np.concatenate([v.reshape(-1, 16).T for v in idx]).astype(np.uint16)


def unstriped8(offs):
    return np.stack([offs[16 * g:16 * g + 16].T.reshape(-1) for g in range(8)]).astype(np.int64)


E2M1 = np.array([0.0, 0.5, 1.0, 1.5, 2.0, 3.0, 4.0, 6.0, -0.0, -0.5, -1.0, -1.5, -2.0, -3.0, -4.0, -6.0])


def pack_weight(w, fmt):
    k, n = w.shape
    w = f64(np.asarray(w, np.float32).astype(ml_dtypes.bfloat16)).reshape(k // 32, 32, n)
    amax = np.abs(w).max(1)
    if fmt == "e4m3":
        byte = np.frexp(amax)[1] - 1 + 127 - 7
    else:
        mant, ex = np.frexp(amax / 6.0)
        byte = np.where(mant > 0.5, ex, ex - 1) + 127
    byte = np.clip(np.where(amax > 0, byte, 1), 1, 254)
    scaled = (w * np.exp2(127.0 - byte)[:, None, :]).reshape(k, n).astype(np.float32)
    by_word = np.ascontiguousarray(scaled.reshape(k // 512, 128, 4, n).transpose(0, 1, 3, 2))
    if fmt == "e4m3":
        words = by_word.astype(ml_dtypes.float8_e4m3fn).view(np.uint8)
    else:
        c = by_word.astype(ml_dtypes.float4_e2m1fn).view(np.uint8) & 0xF
        words = (c[..., 0::2] | (c[..., 1::2] << 4)).reshape(k // 512, 128, 2 * n)
    return np.ascontiguousarray(words), np.ascontiguousarray(byte.astype(np.uint8).reshape(k // 512, 16, n))


def unpack_weight(words, scales, fmt):
    g, _, n = scales.shape
    words = np.ascontiguousarray(words).reshape(g, 128, n, -1)
    if fmt == "e4m3":
        vals = words.view(ml_dtypes.float8_e4m3fn).astype(np.float64)
    else:
        nib = np.empty((g, 128, n, 4), np.uint8)
        nib[..., 0::2] = words & 0xF
        nib[..., 1::2] = words >> 4
        vals = E2M1[nib]
    vals = vals * np.repeat(np.exp2(scales.astype(np.float64) - 127.0), 8, axis=1)[..., None]
    return vals.transpose(0, 1, 3, 2).reshape(g * 512, n)


def silu(v):
    return v / (1.0 + np.exp(-np.maximum(v, -700.0)))


K, M, T, S = 1536, 128, 2048, 1024


def setup_inputs():
    n = np.random.standard_normal
    s = mx_kscale(K)[:, None]
    p_w = pack_weight(n((K, M)) / np.sqrt(K) / s, "e2m1")
    return {
        "xT": (n((K, T)) * s).astype(np.float32),
        "w_words": p_w[0],
        "w_scales": p_w[1],
        "wgt": np.repeat(np.random.uniform(0.5, 2.0, (8, S)), 16, axis=0).astype(np.float32),
        "b": (0.3 * n(128)).astype(np.float32),
        "offs": striped8(np.stack([np.random.permutation(T)[:S] for _ in range(8)])),
    }


def reference(xT, w_words, w_scales, wgt, b, offs):
    idx = unstriped8(offs)
    group = np.arange(K) % 512 // 64
    xg = f64(wgt)[np.arange(K) // 4 % 128] * f64(xT)[np.arange(K)[:, None], idx[group]]
    xT_ = mxq(xg, 0, "e4m3")
    w_ = unpack_weight(w_words, w_scales, "e2m1")
    y = w_.T @ xT_
    return silu(y + f64(b)[:, None])

@@ -1,0 +1,183 @@
+from contextlib import ExitStack
+
+import concourse.mybir as mybir
+
+K, M, T, S = 1536, 128, 2048, 1024
+P = 128
+PACK = 4
+K_PASS = P * PACK
+PASSES = K // K_PASS
+
+FLOPS = 2 * K * M * S
+
+F32 = mybir.dt.float32
+BF16 = mybir.dt.bfloat16
+I32 = mybir.dt.int32
+U32 = mybir.dt.uint32
+U16 = mybir.dt.uint16
+U8 = mybir.dt.uint8
+E4M3X4 = mybir.dt.float8_e4m3fn_x4
+E2M1X4 = mybir.dt.float4_e2m1fn_x4
+MULT = mybir.AluOpType.mult
+SILU = mybir.ActivationFunctionType.Silu
+
+GROUPS = [(0, 512), (512, 128), (640, 128), (768, 128), (896, 128)]
+
+
+def tile_list_heads_silu_kernel(tc, xT, w_words, w_scales, wgt, b, offs, out):
+    nc = tc.nc
+    with ExitStack() as ctx:
+        held = ctx.enter_context(tc.tile_pool(name="held", bufs=1))
+        psum = ctx.enter_context(tc.psum_pool(name="psum", bufs=1))
+
+        lists = held.tile([P, S // 16], U16, name="lists")
+        factors = held.tile([P, S], F32, name="factors", align_bytes=64)
+        compact = held.tile([P, 2, 32], F32, name="compact", align_bytes=64)
+        turned = held.tile([P, 2, 32], F32, name="turned", align_bytes=64)
+        spread = held.tile([P, 32, 2, 16], F32, name="spread", align_bytes=64)
+        planes = [held.tile([P, T], F32, name=f"plane{n}") for n in range(PASSES * PACK)]
+        words = held.tile([P, PASSES, 2 * M], U8, name="words", align_bytes=64)
+        wscales = held.tile([P, PASSES, M], U8, name="wscales", align_bytes=64)
+        bias = held.tile([P, 1], F32, name="bias")
+        warm = held.tile([P, 1], F32, name="warm")
+        codes = held.tile([P, PASSES, S], U32, name="codes", align_bytes=64)
+        scales = held.tile([P, PASSES, S], U8, name="scales", align_bytes=64)
+        result = held.tile([P, S], F32, name="result")
+        sums = [psum.tile([P, width], F32, name=f"sum{first}") for first, width in GROUPS]
+
+        rows = xT.rearrange("(a p i) t -> a i p t", p=P, i=PACK)
+        by_block = wgt.rearrange("(q g s) (b r) -> q s b g r", q=4, g=2, b=32)
+        for q in range(4):
+            queue = nc.sync if q < 2 else nc.scalar
+            queue.dma_start(compact[32 * q : 32 * q + 32], by_block[q, 0])
+        nc.sync.dma_start(lists[:], offs)
+        nc.vector.memset(warm[:], 0.0)
+        nc.scalar.activation(warm[:], warm[:], SILU)
+        nc.vector.memset(wscales[:].rearrange("p a n -> p (a n)").bitcast(I32), 0)
+        for n in range(PASSES * PACK):
+            nc.sync.dma_start(planes[n][:], rows[n // PACK, n % PACK])
+            if n == 5:
+                nc.sync.dma_start(words[:].bitcast(I32), w_words.bitcast(I32).rearrange("a p n -> p a n"))
+                for q in range(4):
+                    nc.sync.dma_start(
+                        wscales[32 * q : 32 * q + 4].bitcast(I32),
+                        w_scales.bitcast(I32)[:, 4 * q : 4 * q + 4].rearrange("a r n -> r a n"),
+                    )
+                nc.sync.dma_start(bias[:], b.unsqueeze(1))
+
+        for g in range(2):
+            nc.vector.transpose(turned[:, g, :], compact[:, g, :])
+        for half, engine in enumerate((nc.vector.tensor_copy, nc.scalar.copy)):
+            blocks = slice(16 * half, 16 * half + 16)
+            engine(
+                spread[:, blocks],
+                turned[:, :, blocks].rearrange("p g b -> p b g").unsqueeze(3).to_broadcast([P, 16, 2, 16]),
+            )
+
+        def spread_factors(half):
+            nc.vector.transpose(
+                factors[:, 512 * half : 512 * half + 512],
+                spread[:, 16 * half : 16 * half + 16].rearrange("p b g s -> p (b g s)"),
+            )
+
+        def gather(slab, i):
+            a, first, width, picked, grouped = slab
+            nc.vector.tensor_tensor(
+                picked[:, i, :],
+                planes[PACK * a + i][:].indirect(lists[:, first // 16 : (first + width) // 16]),
+                factors[:, first : first + width],
+                MULT,
+            )
+
+        def interleave(copy, slab, begin, end):
+            a, first, width, picked, grouped = slab
+            copy(
+                grouped[:, first + begin : first + end].rearrange("p (c i) t -> p c t i", i=4),
+                picked[:, :, begin:end].rearrange("p t (c i) -> p c t i", i=4),
+            )
+
+        def quantise(a, begin, end):
+            nc.vector.quantize_mx(
+                out=codes[:, a, begin:end].bitcast(E4M3X4),
+                scales=scales[:, a, begin:end],
+                in_=passes[a][:, begin:end].rearrange("p c t -> p (c t)"),
+            )
+
+        def multiply(a, groups):
+            for g in groups:
+                first, width = GROUPS[g]
+                cols = slice(first, first + width)
+                nc.tensor.matmul_mx(
+                    out=sums[g][:],
+                    lhsT=words[:, a, :].bitcast(E2M1X4),
+                    lhsT_scale=wscales[:, a, :],
+                    rhs=codes[:, a, cols].bitcast(E4M3X4),
+                    rhs_scale=scales[:, a, cols],
+                    start=(a == 0),
+                    stop=(a == PASSES - 1),
+                )
+
+        def finish(groups, queue):
+            for g in groups:
+                first, width = GROUPS[g]
+                nc.scalar.activation(result[:, first : first + width], sums[g][:], SILU, bias=bias[:])
+            begin, end = GROUPS[groups[0]][0], sum(GROUPS[groups[-1]])
+            queue.dma_start(out[:, begin:end], result[:, begin:end])
+
+        passes = [held.tile([P, S, PACK], BF16, name=f"grouped{a}", align_bytes=64) for a in range(PASSES)]
+
+        def slab(a, first, width):
+            picked = held.tile([P, PACK, width], F32, name=f"picked{a}_{first}")
+            return a, first, width, picked, passes[a]
+
+        s00, s01 = slab(0, 0, 512), slab(0, 512, 512)
+        s10, s11 = slab(1, 0, 512), slab(1, 512, 512)
+        s20, s21, s22 = slab(2, 0, 640), slab(2, 640, 256), slab(2, 896, 128)
+        on_scalar, on_vector = nc.scalar.copy, nc.vector.tensor_copy
+
+        for i in range(PACK):
+            for h, s in enumerate((s00, s01)):
+                if i == 0:
+                    spread_factors(h)
+                gather(s, i)
+        interleave(on_scalar, s00, 0, 512)
+        interleave(on_scalar, s01, 0, 512)
+
+        for i in range(PACK):
+            gather(s10, i)
+            gather(s11, i)
+            if i == 2:
+                quantise(0, 0, 1024)
+                multiply(0, [0, 1, 2, 3, 4])
+        interleave(on_scalar, s10, 0, 512)
+        interleave(on_scalar, s11, 0, 512)
+
+        for i in range(3):
+            gather(s20, i)
+        gather(s21, 0)
+        quantise(1, 0, 1024)
+        multiply(1, [0, 1, 2, 3, 4])
+        gather(s20, 3)
+        interleave(on_scalar, s20, 0, 512)
+        interleave(on_scalar, s20, 512, 640)
+
+        gather(s21, 1)
+        gather(s21, 2)
+        quantise(2, 0, 512)
+        multiply(2, [0])
+        gather(s21, 3)
+        interleave(on_scalar, s21, 0, 256)
+        finish([0], nc.sync)
+        quantise(2, 512, 640)
+        multiply(2, [1])
+        for i in range(3):
+            gather(s22, i)
+        finish([1], nc.sync)
+        quantise(2, 640, 896)
+        multiply(2, [2, 3])
+        gather(s22, 3)
+        interleave(on_vector, s22, 0, 128)
+        finish([2, 3], nc.sync)
+        quantise(2, 896, 1024)
+        multiply(2, [4])
+        finish([4], nc.scalar)

@@ -130,27 +130,22 @@ def tile_list_heads_silu_kernel(tc, xT, w_words, w_scales, wgt, b, offs, out):
             picked = held.tile([P, PACK, width], F32, name=f"picked{a}_{first}")
             return a, first, width, picked, passes[a]
 
-        s00, s01 = slab(0, 0, 512), slab(0, 512, 512)
-        s10, s11 = slab(1, 0, 512), slab(1, 512, 512)
+        s0, s1 = slab(0, 0, S), slab(1, 0, S)
         s20, s21, s22 = slab(2, 0, 640), slab(2, 640, 256), slab(2, 896, 128)
         on_scalar, on_vector = nc.scalar.copy, nc.vector.tensor_copy
 
+        spread_factors(0)
+        spread_factors(1)
         for i in range(PACK):
-            for h, s in enumerate((s00, s01)):
-                if i == 0:
-                    spread_factors(h)
-                gather(s, i)
-        interleave(on_scalar, s00, 0, 512)
-        interleave(on_scalar, s01, 0, 512)
+            gather(s0, i)
+        interleave(on_scalar, s0, 0, S)
 
         for i in range(PACK):
-            gather(s10, i)
-            gather(s11, i)
+            gather(s1, i)
             if i == 2:
                 quantise(0, 0, 1024)
                 multiply(0, [0, 1, 2, 3, 4])
-        interleave(on_scalar, s10, 0, 512)
-        interleave(on_scalar, s11, 0, 512)
+        interleave(on_scalar, s1, 0, S)
 
         for i in range(3):
             gather(s20, i)

@@ -7,6 +7,7 @@ P = 128
 PACK = 4
 K_PASS = P * PACK
 PASSES = K // K_PASS
+LAST = PASSES - 1
 
 FLOPS = 2 * K * M * S
 
@@ -21,7 +22,27 @@ E2M1X4 = mybir.dt.float4_e2m1fn_x4
 MULT = mybir.AluOpType.mult
 SILU = mybir.ActivationFunctionType.Silu
 
-GROUPS = [(0, 512), (512, 128), (640, 128), (768, 128), (896, 128)]
+WIDTHS = [256, 256, 256, 256]
+CALLS = [1024, 1024, 512, 512]
+BANK_ENDS = [512, 768, 1024]
+
+
+def lay_out():
+    calls, place, early, late = [], 0, 0, 0
+    for width, call in zip(WIDTHS, CALLS):
+        pieces, stop = [], early + call - width
+        while early < stop:
+            a, begin = divmod(early, S)
+            end = min(S, begin + stop - early)
+            pieces.append((a, begin, end, place))
+            place += end - begin
+            early += end - begin
+        pieces.append((LAST, late, late + width, place))
+        place += width
+        late += width
+        calls.append(pieces)
+    assert early == LAST * S and late == S
+    return calls
 
 
 def tile_list_heads_silu_kernel(tc, xT, w_words, w_scales, wgt, b, offs, out):
@@ -34,145 +55,104 @@ def tile_list_heads_silu_kernel(tc, xT, w_words, w_scales, wgt, b, offs, out):
         factors = held.tile([P, S], F32, name="factors", align_bytes=64)
         compact = held.tile([P, 2, 32], F32, name="compact", align_bytes=64)
         turned = held.tile([P, 2, 32], F32, name="turned", align_bytes=64)
-        spread = held.tile([P, 32, 2, 16], F32, name="spread", align_bytes=64)
+        spread = held.tile([P, 16, 2, 2, 16], F32, name="spread", align_bytes=64)
         planes = [held.tile([P, T], F32, name=f"plane{n}") for n in range(PASSES * PACK)]
         words = held.tile([P, PASSES, 2 * M], U8, name="words", align_bytes=64)
         wscales = held.tile([P, PASSES, M], U8, name="wscales", align_bytes=64)
         bias = held.tile([P, 1], F32, name="bias")
         warm = held.tile([P, 1], F32, name="warm")
-        codes = held.tile([P, PASSES, S], U32, name="codes", align_bytes=64)
-        scales = held.tile([P, PASSES, S], U8, name="scales", align_bytes=64)
+        picked = [held.tile([P, PACK, S], F32, name=f"picked{a}") for a in range(PASSES)]
+        grouped = held.tile([P, PASSES * S * PACK], BF16, name="grouped", align_bytes=64)
+        codes = held.tile([P, PASSES * S], U32, name="codes", align_bytes=64)
+        scales = held.tile([P, PASSES * S], U8, name="scales", align_bytes=64)
         result = held.tile([P, S], F32, name="result")
-        sums = [psum.tile([P, width], F32, name=f"sum{first}") for first, width in GROUPS]
+        banks = list(zip([0] + BANK_ENDS[:-1], BANK_ENDS))
+        sums = [psum.tile([P, end - begin], F32, name=f"sum{begin}") for begin, end in banks]
+        calls = lay_out()
 
         rows = xT.rearrange("(a p i) t -> a i p t", p=P, i=PACK)
-        by_block = wgt.rearrange("(q g s) (b r) -> q s b g r", q=4, g=2, b=32)
-        for q in range(4):
-            queue = nc.sync if q < 2 else nc.scalar
-            queue.dma_start(compact[32 * q : 32 * q + 32], by_block[q, 0])
+        nc.scalar.dma_start(
+            compact[:].rearrange("p h r -> p (h r)"),
+            wgt.rearrange("(g s) (b r) -> s g b r", s=16, b=16)[0],
+        )
         nc.sync.dma_start(lists[:], offs)
-        nc.vector.memset(warm[:], 0.0)
+        nc.gpsimd.memset(warm[:], 0.0)
         nc.scalar.activation(warm[:], warm[:], SILU)
-        nc.vector.memset(wscales[:].rearrange("p a n -> p (a n)").bitcast(I32), 0)
+        nc.gpsimd.memset(wscales[:].rearrange("p a n -> p (a n)").bitcast(I32), 0)
         for n in range(PASSES * PACK):
             nc.sync.dma_start(planes[n][:], rows[n // PACK, n % PACK])
-            if n == 5:
-                nc.sync.dma_start(words[:].bitcast(I32), w_words.bitcast(I32).rearrange("a p n -> p a n"))
-                for q in range(4):
-                    nc.sync.dma_start(
-                        wscales[32 * q : 32 * q + 4].bitcast(I32),
-                        w_scales.bitcast(I32)[:, 4 * q : 4 * q + 4].rearrange("a r n -> r a n"),
-                    )
-                nc.sync.dma_start(bias[:], b.unsqueeze(1))
-
-        for g in range(2):
-            nc.vector.transpose(turned[:, g, :], compact[:, g, :])
-        for half, engine in enumerate((nc.vector.tensor_copy, nc.scalar.copy)):
-            blocks = slice(16 * half, 16 * half + 16)
-            engine(
-                spread[:, blocks],
-                turned[:, :, blocks].rearrange("p g b -> p b g").unsqueeze(3).to_broadcast([P, 16, 2, 16]),
+        nc.sync.dma_start(words[:].bitcast(I32), w_words.bitcast(I32).rearrange("a p n -> p a n"))
+        for q in range(4):
+            nc.sync.dma_start(
+                wscales[32 * q : 32 * q + 4].bitcast(I32),
+                w_scales.bitcast(I32)[:, 4 * q : 4 * q + 4].rearrange("a r n -> r a n"),
             )
+        nc.sync.dma_start(bias[:], b.unsqueeze(1))
 
-        def spread_factors(half):
+        for h in range(2):
+            nc.vector.transpose(turned[:, h, :], compact[:, h, :])
+        by_block = turned[:].rearrange("p h (g b) -> p b h g", g=2)
+        for half, engine in enumerate((nc.vector.tensor_copy, nc.scalar.copy)):
+            blocks = slice(8 * half, 8 * half + 8)
+            engine(spread[:, blocks], by_block[:, blocks].unsqueeze(4).to_broadcast([P, 8, 2, 2, 16]))
+        for half in range(2):
             nc.vector.transpose(
                 factors[:, 512 * half : 512 * half + 512],
-                spread[:, 16 * half : 16 * half + 16].rearrange("p b g s -> p (b g s)"),
+                spread[:, 8 * half : 8 * half + 8].rearrange("p b h g s -> p (b h g s)"),
             )
 
-        def gather(slab, i):
-            a, first, width, picked, grouped = slab
+        def gather(a, i, begin, end):
             nc.vector.tensor_tensor(
-                picked[:, i, :],
-                planes[PACK * a + i][:].indirect(lists[:, first // 16 : (first + width) // 16]),
-                factors[:, first : first + width],
+                picked[a][:, i, begin:end],
+                planes[PACK * a + i][:].indirect(lists[:, begin // 16 : end // 16]),
+                factors[:, begin:end],
                 MULT,
             )
 
-        def interleave(copy, slab, begin, end):
-            a, first, width, picked, grouped = slab
-            copy(
-                grouped[:, first + begin : first + end].rearrange("p (c i) t -> p c t i", i=4),
-                picked[:, :, begin:end].rearrange("p t (c i) -> p c t i", i=4),
+        def interleave(a, begin, end, place):
+            nc.scalar.copy(
+                grouped[:, PACK * place : PACK * (place + end - begin)].rearrange("p (c i t) -> p c t i", i=4, t=PACK),
+                picked[a][:, :, begin:end].rearrange("p t (c i) -> p c t i", i=4),
             )
 
-        def quantise(a, begin, end):
+        for a in range(LAST):
+            for i in range(PACK):
+                gather(a, i, 0, S)
+            for piece in [piece for call in calls for piece in call if piece[0] == a]:
+                interleave(*piece)
+        for i in range(PACK - 1):
+            gather(LAST, i, 0, S)
+        for call in calls:
+            gather(LAST, PACK - 1, call[-1][1], call[-1][2])
+            interleave(*call[-1])
+
+        missing = [PASSES * (end - begin) for begin, end in banks]
+        for call in calls:
+            first, stop = call[0][3], call[-1][3] + call[-1][2] - call[-1][1]
             nc.vector.quantize_mx(
-                out=codes[:, a, begin:end].bitcast(E4M3X4),
-                scales=scales[:, a, begin:end],
-                in_=passes[a][:, begin:end].rearrange("p c t -> p (c t)"),
+                out=codes[:, first:stop].bitcast(E4M3X4),
+                scales=scales[:, first:stop],
+                in_=grouped[:, PACK * first : PACK * stop],
             )
-
-        def multiply(a, groups):
-            for g in groups:
-                first, width = GROUPS[g]
-                cols = slice(first, first + width)
-                nc.tensor.matmul_mx(
-                    out=sums[g][:],
-                    lhsT=words[:, a, :].bitcast(E2M1X4),
-                    lhsT_scale=wscales[:, a, :],
-                    rhs=codes[:, a, cols].bitcast(E4M3X4),
-                    rhs_scale=scales[:, a, cols],
-                    start=(a == 0),
-                    stop=(a == PASSES - 1),
-                )
-
-        def finish(groups, queue):
-            for g in groups:
-                first, width = GROUPS[g]
-                nc.scalar.activation(result[:, first : first + width], sums[g][:], SILU, bias=bias[:])
-            begin, end = GROUPS[groups[0]][0], sum(GROUPS[groups[-1]])
-            queue.dma_start(out[:, begin:end], result[:, begin:end])
-
-        passes = [held.tile([P, S, PACK], BF16, name=f"grouped{a}", align_bytes=64) for a in range(PASSES)]
-
-        def slab(a, first, width):
-            picked = held.tile([P, PACK, width], F32, name=f"picked{a}_{first}")
-            return a, first, width, picked, passes[a]
-
-        s0, s1 = slab(0, 0, S), slab(1, 0, S)
-        s20, s21, s22 = slab(2, 0, 640), slab(2, 640, 256), slab(2, 896, 128)
-        on_scalar, on_vector = nc.scalar.copy, nc.vector.tensor_copy
-
-        spread_factors(0)
-        spread_factors(1)
-        for i in range(PACK):
-            gather(s0, i)
-        interleave(on_scalar, s0, 0, S)
-
-        for i in range(PACK):
-            gather(s1, i)
-            if i == 2:
-                quantise(0, 0, 1024)
-                multiply(0, [0, 1, 2, 3, 4])
-        interleave(on_scalar, s1, 0, S)
-
-        for i in range(3):
-            gather(s20, i)
-        gather(s21, 0)
-        quantise(1, 0, 1024)
-        multiply(1, [0, 1, 2, 3, 4])
-        gather(s20, 3)
-        interleave(on_scalar, s20, 0, 512)
-        interleave(on_scalar, s20, 512, 640)
-
-        gather(s21, 1)
-        gather(s21, 2)
-        quantise(2, 0, 512)
-        multiply(2, [0])
-        gather(s21, 3)
-        interleave(on_scalar, s21, 0, 256)
-        finish([0], nc.sync)
-        quantise(2, 512, 640)
-        multiply(2, [1])
-        for i in range(3):
-            gather(s22, i)
-        finish([1], nc.sync)
-        quantise(2, 640, 896)
-        multiply(2, [2, 3])
-        gather(s22, 3)
-        interleave(on_vector, s22, 0, 128)
-        finish([2, 3], nc.sync)
-        quantise(2, 896, 1024)
-        multiply(2, [4])
-        finish([4], nc.scalar)
+            for bank, (left, right) in enumerate(banks):
+                was_open = missing[bank] > 0
+                for a, begin, end, place in call:
+                    low, high = max(begin, left), min(end, right)
+                    step = 512 if high - low == 512 else 128
+                    for column in range(low, high, step):
+                        cols = slice(place + column - begin, place + column - begin + step)
+                        opens = missing[bank] == PASSES * (right - left)
+                        missing[bank] -= step
+                        nc.tensor.matmul_mx(
+                            out=sums[bank][:, column - left : column - left + step],
+                            lhsT=words[:, a, :].bitcast(E2M1X4),
+                            lhsT_scale=wscales[:, a, :],
+                            rhs=codes[:, cols].bitcast(E4M3X4),
+                            rhs_scale=scales[:, cols],
+                            start=opens,
+                            stop=missing[bank] == 0,
+                        )
+                if was_open and missing[bank] == 0:
+                    nc.scalar.activation(result[:, left:right], sums[bank][:], SILU, bias=bias[:])
+                    queue = nc.scalar if right == S else nc.sync
+                    queue.dma_start(out[:, left:right], result[:, left:right])

@@ -56,7 +56,7 @@ def tile_list_heads_silu_kernel(tc, xT, w_words, w_scales, wgt, b, offs, out):
         compact = held.tile([P, 2, 32], F32, name="compact", align_bytes=64)
         turned = held.tile([P, 2, 32], F32, name="turned", align_bytes=64)
         spread = held.tile([P, 16, 2, 2, 16], F32, name="spread", align_bytes=64)
-        planes = [held.tile([P, T], F32, name=f"plane{n}") for n in range(PASSES * PACK)]
+        planes = [held.tile([P, T], F32, name=f"plane{n}", align_bytes=256) for n in range(PASSES * PACK)]
         words = held.tile([P, PASSES, 2 * M], U8, name="words", align_bytes=64)
         wscales = held.tile([P, PASSES, M], U8, name="wscales", align_bytes=64)
         bias = held.tile([P, 1], F32, name="bias")
@@ -76,9 +76,9 @@ def tile_list_heads_silu_kernel(tc, xT, w_words, w_scales, wgt, b, offs, out):
             wgt.rearrange("(g s) (b r) -> s g b r", s=16, b=16)[0],
         )
         nc.sync.dma_start(lists[:], offs)
-        nc.gpsimd.memset(warm[:], 0.0)
+        nc.vector.memset(warm[:], 0.0)
         nc.scalar.activation(warm[:], warm[:], SILU)
-        nc.gpsimd.memset(wscales[:].rearrange("p a n -> p (a n)").bitcast(I32), 0)
+        nc.vector.memset(wscales[:].rearrange("p a n -> p (a n)").bitcast(I32), 0)
         for n in range(PASSES * PACK):
             nc.sync.dma_start(planes[n][:], rows[n // PACK, n % PACK])
         nc.sync.dma_start(words[:].bitcast(I32), w_words.bitcast(I32).rearrange("a p n -> p a n"))

@@ -22,9 +22,9 @@ E2M1X4 = mybir.dt.float4_e2m1fn_x4
 MULT = mybir.AluOpType.mult
 SILU = mybir.ActivationFunctionType.Silu
 
-WIDTHS = [256, 256, 256, 256]
-CALLS = [1024, 1024, 512, 512]
-BANK_ENDS = [512, 768, 1024]
+WIDTHS = [0, 128, 256, 256, 256, 128]
+CALLS = [512, 1024, 512, 512, 256, 256]
+BANK_ENDS = [384, 640, 896, 1024]
 
 
 def lay_out():
@@ -37,7 +37,8 @@ def lay_out():
             pieces.append((a, begin, end, place))
             place += end - begin
             early += end - begin
-        pieces.append((LAST, late, late + width, place))
+        if width:
+            pieces.append((LAST, late, late + width, place))
         place += width
         late += width
         calls.append(pieces)
@@ -109,22 +110,29 @@ def tile_list_heads_silu_kernel(tc, xT, w_words, w_scales, wgt, b, offs, out):
                 MULT,
             )
 
-        def interleave(a, begin, end, place):
+        def interleave(a, begin, end, place, rows=slice(0, PACK)):
+            room = grouped[:, PACK * place : PACK * (place + end - begin)]
             nc.scalar.copy(
-                grouped[:, PACK * place : PACK * (place + end - begin)].rearrange("p (c i t) -> p c t i", i=4, t=PACK),
-                picked[a][:, :, begin:end].rearrange("p t (c i) -> p c t i", i=4),
+                room.rearrange("p (c i t) -> p c t i", i=4, t=PACK)[:, :, rows],
+                picked[a][:, rows, begin:end].rearrange("p t (c i) -> p c t i", i=4),
             )
 
-        for a in range(LAST):
-            for i in range(PACK):
-                gather(a, i, 0, S)
-            for piece in [piece for call in calls for piece in call if piece[0] == a]:
-                interleave(*piece)
-        for i in range(PACK - 1):
-            gather(LAST, i, 0, S)
-        for call in calls:
+        pairs = (slice(0, 2), slice(2, PACK))
+        for a in range(PASSES):
+            pieces = [piece for call in calls for piece in call if piece[0] == a]
+            for rows in pairs:
+                for i in range(rows.start, rows.stop):
+                    if (a, i) == (LAST, 1):
+                        for begin in range(0, S, 512):
+                            gather(a, i, begin, begin + 512)
+                    elif (a, i) != (LAST, PACK - 1):
+                        gather(a, i, 0, S)
+                if (a, rows) != (LAST, pairs[1]):
+                    for piece in pieces:
+                        interleave(*piece, rows)
+        for call in [call for call in calls if call[-1][0] == LAST]:
             gather(LAST, PACK - 1, call[-1][1], call[-1][2])
-            interleave(*call[-1])
+            interleave(*call[-1], pairs[1])
 
         missing = [PASSES * (end - begin) for begin, end in banks]
         for call in calls:

@@ -22,8 +22,8 @@ E2M1X4 = mybir.dt.float4_e2m1fn_x4
 MULT = mybir.AluOpType.mult
 SILU = mybir.ActivationFunctionType.Silu
 
-WIDTHS = [0, 128, 256, 256, 256, 128]
-CALLS = [512, 1024, 512, 512, 256, 256]
+WIDTHS = [0, 0, 128, 256, 256, 256, 128]
+CALLS = [512, 256, 512, 512, 512, 512, 256]
 BANK_ENDS = [384, 640, 896, 1024]
 
 

@@ -28,21 +28,25 @@ BANK_ENDS = [384, 640, 896, 1024]
 
 
 def lay_out():
-    calls, place, early, late = [], 0, 0, 0
+    ahead = sum(call for width, call in zip(WIDTHS, CALLS) if width == 0)
+    units = [(0, column) for column in range(0, ahead, 128)]
+    units += [(a, column) for column in range(0, S, 128) for a in range(LAST) if (a, column) not in units]
+    calls, place, late = [], 0, 0
     for width, call in zip(WIDTHS, CALLS):
-        pieces, stop = [], early + call - width
-        while early < stop:
-            a, begin = divmod(early, S)
-            end = min(S, begin + stop - early)
-            pieces.append((a, begin, end, place))
-            place += end - begin
-            early += end - begin
+        pieces = []
+        for a, column in sorted(units[: (call - width) // 128]):
+            if pieces and pieces[-1][0] == a and pieces[-1][2] == column:
+                pieces[-1] = (a, pieces[-1][1], column + 128, pieces[-1][3])
+            else:
+                pieces.append((a, column, column + 128, place))
+            place += 128
+        units = units[(call - width) // 128 :]
         if width:
             pieces.append((LAST, late, late + width, place))
         place += width
         late += width
         calls.append(pieces)
-    assert early == LAST * S and late == S
+    assert not units and late == S
     return calls
 
 
@@ -72,16 +76,17 @@ def tile_list_heads_silu_kernel(tc, xT, w_words, w_scales, wgt, b, offs, out):
         calls = lay_out()
 
         rows = xT.rearrange("(a p i) t -> a i p t", p=P, i=PACK)
-        nc.scalar.dma_start(
+        nc.sync.dma_start(
             compact[:].rearrange("p h r -> p (h r)"),
             wgt.rearrange("(g s) (b r) -> s g b r", s=16, b=16)[0],
         )
-        nc.sync.dma_start(lists[:], offs)
         nc.vector.memset(warm[:], 0.0)
         nc.scalar.activation(warm[:], warm[:], SILU)
         nc.vector.memset(wscales[:].rearrange("p a n -> p (a n)").bitcast(I32), 0)
         for n in range(PASSES * PACK):
             nc.sync.dma_start(planes[n][:], rows[n // PACK, n % PACK])
+            if n == 0:
+                nc.sync.dma_start(lists[:], offs)
         nc.sync.dma_start(words[:].bitcast(I32), w_words.bitcast(I32).rearrange("a p n -> p a n"))
         for q in range(4):
             nc.sync.dma_start(
@@ -110,9 +115,9 @@ def tile_list_heads_silu_kernel(tc, xT, w_words, w_scales, wgt, b, offs, out):
                 MULT,
             )
 
-        def interleave(a, begin, end, place, rows=slice(0, PACK)):
+        def interleave(a, begin, end, place, rows, copy=nc.scalar.copy):
             room = grouped[:, PACK * place : PACK * (place + end - begin)]
-            nc.scalar.copy(
+            copy(
                 room.rearrange("p (c i t) -> p c t i", i=4, t=PACK)[:, :, rows],
                 picked[a][:, rows, begin:end].rearrange("p t (c i) -> p c t i", i=4),
             )
@@ -123,8 +128,8 @@ def tile_list_heads_silu_kernel(tc, xT, w_words, w_scales, wgt, b, offs, out):
             for rows in pairs:
                 for i in range(rows.start, rows.stop):
                     if (a, i) == (LAST, 1):
-                        for begin in range(0, S, 512):
-                            gather(a, i, begin, begin + 512)
+                        for begin in range(0, S, 1024):
+                            gather(a, i, begin, begin + 1024)
                     elif (a, i) != (LAST, PACK - 1):
                         gather(a, i, 0, S)
                 if (a, rows) != (LAST, pairs[1]):

@@ -25,6 +25,7 @@ SILU = mybir.ActivationFunctionType.Silu
 WIDTHS = [0, 0, 128, 256, 256, 256, 128]
 CALLS = [512, 256, 512, 512, 512, 512, 256]
 BANK_ENDS = [384, 640, 896, 1024]
+STORE_ENDS = [384, 640, 1024]
 
 
 def lay_out():
@@ -167,5 +168,7 @@ def tile_list_heads_silu_kernel(tc, xT, w_words, w_scales, wgt, b, offs, out):
                         )
                 if was_open and missing[bank] == 0:
                     nc.scalar.activation(result[:, left:right], sums[bank][:], SILU, bias=bias[:])
-                    queue = nc.scalar if right == S else nc.sync
-                    queue.dma_start(out[:, left:right], result[:, left:right])
+                    if right in STORE_ENDS:
+                        low = max(end for end in [0] + STORE_ENDS if end < right)
+                        queue = nc.scalar if right == S else nc.sync
+                        queue.dma_start(out[:, low:right], result[:, low:right])

@@ -5,9 +5,9 @@ import concourse.mybir as mybir
 K, M, T, S = 1536, 128, 2048, 1024
 P = 128
 PACK = 4
-K_PASS = P * PACK
-PASSES = K // K_PASS
+PASSES = K // (P * PACK)
 LAST = PASSES - 1
+STEP = 128
 
 FLOPS = 2 * K * M * S
 
@@ -22,32 +22,34 @@ E2M1X4 = mybir.dt.float4_e2m1fn_x4
 MULT = mybir.AluOpType.mult
 SILU = mybir.ActivationFunctionType.Silu
 
-WIDTHS = [0, 0, 128, 256, 256, 256, 128]
-CALLS = [512, 256, 512, 512, 512, 512, 256]
+EARLY_CALLS = [512, 256]
+RANGES = [128, 256, 256, 256, 128]
+LATE_CALLS = [512, 512, 512, 512, 256]
 BANK_ENDS = [384, 640, 896, 1024]
 STORE_ENDS = [384, 640, 1024]
 
 
-def lay_out():
-    ahead = sum(call for width, call in zip(WIDTHS, CALLS) if width == 0)
-    units = [(0, column) for column in range(0, ahead, 128)]
-    units += [(a, column) for column in range(0, S, 128) for a in range(LAST) if (a, column) not in units]
+def deal_columns():
+    ahead = sum(EARLY_CALLS)
+    waiting = [(0, column) for column in range(0, ahead, STEP)]
+    waiting += [(a, column) for column in range(0, S, STEP) for a in range(LAST) if a > 0 or column >= ahead]
     calls, place, late = [], 0, 0
-    for width, call in zip(WIDTHS, CALLS):
+    for width, call in zip([0] * len(EARLY_CALLS) + RANGES, EARLY_CALLS + LATE_CALLS):
+        count = (call - width) // STEP
         pieces = []
-        for a, column in sorted(units[: (call - width) // 128]):
+        for a, column in sorted(waiting[:count]):
             if pieces and pieces[-1][0] == a and pieces[-1][2] == column:
-                pieces[-1] = (a, pieces[-1][1], column + 128, pieces[-1][3])
+                pieces[-1] = (a, pieces[-1][1], column + STEP, pieces[-1][3])
             else:
-                pieces.append((a, column, column + 128, place))
-            place += 128
-        units = units[(call - width) // 128 :]
+                pieces.append((a, column, column + STEP, place))
+            place += STEP
+        waiting = waiting[count:]
         if width:
             pieces.append((LAST, late, late + width, place))
         place += width
         late += width
         calls.append(pieces)
-    assert not units and late == S
+    assert not waiting and late == S
     return calls
 
 
@@ -58,25 +60,25 @@ def tile_list_heads_silu_kernel(tc, xT, w_words, w_scales, wgt, b, offs, out):
         psum = ctx.enter_context(tc.psum_pool(name="psum", bufs=1))
 
         lists = held.tile([P, S // 16], U16, name="lists")
-        factors = held.tile([P, S], F32, name="factors", align_bytes=64)
-        compact = held.tile([P, 2, 32], F32, name="compact", align_bytes=64)
-        turned = held.tile([P, 2, 32], F32, name="turned", align_bytes=64)
-        spread = held.tile([P, 16, 2, 2, 16], F32, name="spread", align_bytes=64)
+        factors = held.tile([P, S], F32, name="factors", align_bytes=256)
+        compact = held.tile([P, 2, 32], F32, name="compact", align_bytes=256)
+        turned = held.tile([P, 2, 32], F32, name="turned", align_bytes=256)
+        spread = held.tile([P, 16, 2, 2, 16], F32, name="spread", align_bytes=256)
         planes = [held.tile([P, T], F32, name=f"plane{n}", align_bytes=256) for n in range(PASSES * PACK)]
-        words = held.tile([P, PASSES, 2 * M], U8, name="words", align_bytes=64)
-        wscales = held.tile([P, PASSES, M], U8, name="wscales", align_bytes=64)
+        words = held.tile([P, PASSES, 2 * M], U8, name="words", align_bytes=256)
+        wscales = held.tile([P, PASSES, M], U8, name="wscales", align_bytes=256)
         bias = held.tile([P, 1], F32, name="bias")
         warm = held.tile([P, 1], F32, name="warm")
-        picked = [held.tile([P, PACK, S], F32, name=f"picked{a}") for a in range(PASSES)]
-        grouped = held.tile([P, PASSES * S * PACK], BF16, name="grouped", align_bytes=64)
-        codes = held.tile([P, PASSES * S], U32, name="codes", align_bytes=64)
-        scales = held.tile([P, PASSES * S], U8, name="scales", align_bytes=64)
+        picked = [held.tile([P, PACK, S], F32, name=f"picked{a}", align_bytes=256) for a in range(PASSES)]
+        rounded = held.tile([P, PASSES * S * PACK], BF16, name="rounded", align_bytes=256)
+        codes = held.tile([P, PASSES * S], U32, name="codes", align_bytes=256)
+        scales = held.tile([P, PASSES * S], U8, name="scales", align_bytes=256)
         result = held.tile([P, S], F32, name="result")
         banks = list(zip([0] + BANK_ENDS[:-1], BANK_ENDS))
         sums = [psum.tile([P, end - begin], F32, name=f"sum{begin}") for begin, end in banks]
-        calls = lay_out()
+        calls = deal_columns()
 
-        rows = xT.rearrange("(a p i) t -> a i p t", p=P, i=PACK)
+        by_plane = xT.rearrange("(a p i) t -> a i p t", p=P, i=PACK)
         nc.sync.dma_start(
             compact[:].rearrange("p h r -> p (h r)"),
             wgt.rearrange("(g s) (b r) -> s g b r", s=16, b=16)[0],
@@ -85,7 +87,7 @@ def tile_list_heads_silu_kernel(tc, xT, w_words, w_scales, wgt, b, offs, out):
         nc.scalar.activation(warm[:], warm[:], SILU)
         nc.vector.memset(wscales[:].rearrange("p a n -> p (a n)").bitcast(I32), 0)
         for n in range(PASSES * PACK):
-            nc.sync.dma_start(planes[n][:], rows[n // PACK, n % PACK])
+            nc.sync.dma_start(planes[n][:], by_plane[n // PACK, n % PACK])
             if n == 0:
                 nc.sync.dma_start(lists[:], offs)
         nc.sync.dma_start(words[:].bitcast(I32), w_words.bitcast(I32).rearrange("a p n -> p a n"))
@@ -99,9 +101,9 @@ def tile_list_heads_silu_kernel(tc, xT, w_words, w_scales, wgt, b, offs, out):
         for h in range(2):
             nc.vector.transpose(turned[:, h, :], compact[:, h, :])
         by_block = turned[:].rearrange("p h (g b) -> p b h g", g=2)
-        for half, engine in enumerate((nc.vector.tensor_copy, nc.scalar.copy)):
+        for half, copy in enumerate((nc.vector.tensor_copy, nc.scalar.copy)):
             blocks = slice(8 * half, 8 * half + 8)
-            engine(spread[:, blocks], by_block[:, blocks].unsqueeze(4).to_broadcast([P, 8, 2, 2, 16]))
+            copy(spread[:, blocks], by_block[:, blocks].unsqueeze(4).to_broadcast([P, 8, 2, 2, 16]))
         for half in range(2):
             nc.vector.transpose(
                 factors[:, 512 * half : 512 * half + 512],
@@ -116,29 +118,27 @@ def tile_list_heads_silu_kernel(tc, xT, w_words, w_scales, wgt, b, offs, out):
                 MULT,
             )
 
-        def interleave(a, begin, end, place, rows, copy=nc.scalar.copy):
-            room = grouped[:, PACK * place : PACK * (place + end - begin)]
-            copy(
-                room.rearrange("p (c i t) -> p c t i", i=4, t=PACK)[:, :, rows],
-                picked[a][:, rows, begin:end].rearrange("p t (c i) -> p c t i", i=4),
+        def lay_out(a, begin, end, place, pair):
+            room = rounded[:, PACK * place : PACK * (place + end - begin)]
+            nc.scalar.copy(
+                room.rearrange("p (c n i) -> p c i n", n=4, i=PACK)[:, :, pair],
+                picked[a][:, pair, begin:end].rearrange("p i (c n) -> p c i n", n=4),
             )
 
         pairs = (slice(0, 2), slice(2, PACK))
         for a in range(PASSES):
             pieces = [piece for call in calls for piece in call if piece[0] == a]
-            for rows in pairs:
-                for i in range(rows.start, rows.stop):
-                    if (a, i) == (LAST, 1):
-                        for begin in range(0, S, 1024):
-                            gather(a, i, begin, begin + 1024)
-                    elif (a, i) != (LAST, PACK - 1):
-                        gather(a, i, 0, S)
-                if (a, rows) != (LAST, pairs[1]):
+            for pair in pairs:
+                if (a, pair) == (LAST, pairs[1]):
+                    gather(a, pair.start, 0, S)
                     for piece in pieces:
-                        interleave(*piece, rows)
-        for call in [call for call in calls if call[-1][0] == LAST]:
-            gather(LAST, PACK - 1, call[-1][1], call[-1][2])
-            interleave(*call[-1], pairs[1])
+                        gather(a, pair.start + 1, piece[1], piece[2])
+                        lay_out(*piece, pair)
+                else:
+                    gather(a, pair.start, 0, S)
+                    gather(a, pair.start + 1, 0, S)
+                    for piece in pieces:
+                        lay_out(*piece, pair)
 
         missing = [PASSES * (end - begin) for begin, end in banks]
         for call in calls:
@@ -146,19 +146,17 @@ def tile_list_heads_silu_kernel(tc, xT, w_words, w_scales, wgt, b, offs, out):
             nc.vector.quantize_mx(
                 out=codes[:, first:stop].bitcast(E4M3X4),
                 scales=scales[:, first:stop],
-                in_=grouped[:, PACK * first : PACK * stop],
+                in_=rounded[:, PACK * first : PACK * stop],
             )
             for bank, (left, right) in enumerate(banks):
                 was_open = missing[bank] > 0
                 for a, begin, end, place in call:
-                    low, high = max(begin, left), min(end, right)
-                    step = 512 if high - low == 512 else 128
-                    for column in range(low, high, step):
-                        cols = slice(place + column - begin, place + column - begin + step)
+                    for column in range(max(begin, left), min(end, right), STEP):
+                        cols = slice(place + column - begin, place + column - begin + STEP)
                         opens = missing[bank] == PASSES * (right - left)
-                        missing[bank] -= step
+                        missing[bank] -= STEP
                         nc.tensor.matmul_mx(
-                            out=sums[bank][:, column - left : column - left + step],
+                            out=sums[bank][:, column - left : column - left + STEP],
                             lhsT=words[:, a, :].bitcast(E2M1X4),
                             lhsT_scale=wscales[:, a, :],
                             rhs=codes[:, cols].bitcast(E4M3X4),
@@ -169,6 +167,6 @@ def tile_list_heads_silu_kernel(tc, xT, w_words, w_scales, wgt, b, offs, out):
                 if was_open and missing[bank] == 0:
                     nc.scalar.activation(result[:, left:right], sums[bank][:], SILU, bias=bias[:])
                     if right in STORE_ENDS:
-                        low = max(end for end in [0] + STORE_ENDS if end < right)
+                        stored = max(end for end in [0] + STORE_ENDS if end < right)
                         queue = nc.scalar if right == S else nc.sync
-                        queue.dma_start(out[:, low:right], result[:, low:right])
+                        queue.dma_start(out[:, stored:right], result[:, stored:right])

@@ -121,8 +121,8 @@ def tile_list_heads_silu_kernel(tc, xT, w_words, w_scales, wgt, b, offs, out):
         def lay_out(a, begin, end, place, pair):
             room = rounded[:, PACK * place : PACK * (place + end - begin)]
             nc.scalar.copy(
-                room.rearrange("p (c n i) -> p c i n", n=4, i=PACK)[:, :, pair],
-                picked[a][:, pair, begin:end].rearrange("p i (c n) -> p c i n", n=4),
+                room.rearrange("p (c i) -> p c i", i=PACK)[:, :, pair],
+                picked[a][:, pair, begin:end].rearrange("p i c -> p c i"),
             )
 
         pairs = (slice(0, 2), slice(2, PACK))

@@ -26,7 +26,7 @@ EARLY_CALLS = [512, 256]
 RANGES = [128, 256, 256, 256, 128]
 LATE_CALLS = [512, 512, 512, 512, 256]
 BANK_ENDS = [384, 640, 896, 1024]
-STORE_ENDS = [384, 640, 1024]
+STORE_ENDS = [640, 1024]
 
 
 def deal_columns():

@@ -168,5 +168,5 @@ def tile_list_heads_silu_kernel(tc, xT, w_words, w_scales, wgt, b, offs, out):
                     nc.scalar.activation(result[:, left:right], sums[bank][:], SILU, bias=bias[:])
                     if right in STORE_ENDS:
                         stored = max(end for end in [0] + STORE_ENDS if end < right)
-                        queue = nc.scalar if right == S else nc.sync
+                        queue = nc.sync
                         queue.dma_start(out[:, stored:right], result[:, stored:right])

@@ -22,35 +22,37 @@ E2M1X4 = mybir.dt.float4_e2m1fn_x4
 MULT = mybir.AluOpType.mult
 SILU = mybir.ActivationFunctionType.Silu
 
-EARLY_CALLS = [512, 256]
-RANGES = [128, 256, 256, 256, 128]
-LATE_CALLS = [512, 512, 512, 512, 256]
-BANK_ENDS = [384, 640, 896, 1024]
+EARLY_CALLS = [4, 2]
+LATE_CALLS = [4, 2, 2, 2, 2, 2, 2, 2]
+GATHER_ENDS = [384, 640, 1024]
+BANK_ENDS = [384, 640, 768, 896, 1024]
 STORE_ENDS = [640, 1024]
 
 
-def deal_columns():
-    ahead = sum(EARLY_CALLS)
-    waiting = [(0, column) for column in range(0, ahead, STEP)]
-    waiting += [(a, column) for column in range(0, S, STEP) for a in range(LAST) if a > 0 or column >= ahead]
-    calls, place, late = [], 0, 0
-    for width, call in zip([0] * len(EARLY_CALLS) + RANGES, EARLY_CALLS + LATE_CALLS):
-        count = (call - width) // STEP
-        pieces = []
-        for a, column in sorted(waiting[:count]):
-            if pieces and pieces[-1][0] == a and pieces[-1][2] == column:
-                pieces[-1] = (a, pieces[-1][1], column + STEP, pieces[-1][3])
-            else:
-                pieces.append((a, column, column + STEP, place))
-            place += STEP
-        waiting = waiting[count:]
-        if width:
-            pieces.append((LAST, late, late + width, place))
-        place += width
-        late += width
-        calls.append(pieces)
-    assert not waiting and late == S
+def deal_blocks():
+    ahead = sum(EARLY_CALLS) * STEP
+    row = [(0, column) for column in range(0, ahead, STEP)]
+    waiting = [(a, column) for column in range(0, S, STEP) for a in range(LAST) if a > 0 or column >= ahead]
+    for n, width in enumerate(LATE_CALLS):
+        row += sorted(waiting[: width - 1]) + [(LAST, n * STEP)]
+        waiting = waiting[width - 1 :]
+    assert not waiting
+    blocks = [(a, column, n * STEP) for n, (a, column) in enumerate(row)]
+    calls = []
+    for width in EARLY_CALLS + LATE_CALLS:
+        calls.append(blocks[:width])
+        blocks = blocks[width:]
     return calls
+
+
+def runs(blocks):
+    joined = []
+    for a, column, place in blocks:
+        if joined and joined[-1][1] == column and joined[-1][2] + column - joined[-1][0] == place:
+            joined[-1] = (joined[-1][0], column + STEP, joined[-1][2])
+        else:
+            joined.append((column, column + STEP, place))
+    return joined
 
 
 def tile_list_heads_silu_kernel(tc, xT, w_words, w_scales, wgt, b, offs, out):
@@ -76,7 +78,7 @@ def tile_list_heads_silu_kernel(tc, xT, w_words, w_scales, wgt, b, offs, out):
         result = held.tile([P, S], F32, name="result")
         banks = list(zip([0] + BANK_ENDS[:-1], BANK_ENDS))
         sums = [psum.tile([P, end - begin], F32, name=f"sum{begin}") for begin, end in banks]
-        calls = deal_columns()
+        calls = deal_blocks()
 
         by_plane = xT.rearrange("(a p i) t -> a i p t", p=P, i=PACK)
         nc.sync.dma_start(
@@ -127,22 +129,19 @@ def tile_list_heads_silu_kernel(tc, xT, w_words, w_scales, wgt, b, offs, out):
 
         pairs = (slice(0, 2), slice(2, PACK))
         for a in range(PASSES):
-            pieces = [piece for call in calls for piece in call if piece[0] == a]
+            pieces = [piece for call in calls for piece in runs([block for block in call if block[0] == a])]
             for pair in pairs:
-                if (a, pair) == (LAST, pairs[1]):
-                    gather(a, pair.start, 0, S)
+                gather(a, pair.start, 0, S)
+                ends = GATHER_ENDS if (a, pair) == (LAST, pairs[1]) else [S]
+                for begin, end in zip([0] + ends[:-1], ends):
+                    gather(a, pair.start + 1, begin, end)
                     for piece in pieces:
-                        gather(a, pair.start + 1, piece[1], piece[2])
-                        lay_out(*piece, pair)
-                else:
-                    gather(a, pair.start, 0, S)
-                    gather(a, pair.start + 1, 0, S)
-                    for piece in pieces:
-                        lay_out(*piece, pair)
+                        if begin <= piece[0] < end:
+                            lay_out(a, *piece, pair)
 
         missing = [PASSES * (end - begin) for begin, end in banks]
         for call in calls:
-            first, stop = call[0][3], call[-1][3] + call[-1][2] - call[-1][1]
+            first, stop = call[0][2], call[-1][2] + STEP
             nc.vector.quantize_mx(
                 out=codes[:, first:stop].bitcast(E4M3X4),
                 scales=scales[:, first:stop],
@@ -150,9 +149,9 @@ def tile_list_heads_silu_kernel(tc, xT, w_words, w_scales, wgt, b, offs, out):
             )
             for bank, (left, right) in enumerate(banks):
                 was_open = missing[bank] > 0
-                for a, begin, end, place in call:
-                    for column in range(max(begin, left), min(end, right), STEP):
-                        cols = slice(place + column - begin, place + column - begin + STEP)
+                for a, column, place in call:
+                    if left <= column < right:
+                        cols = slice(place, place + STEP)
                         opens = missing[bank] == PASSES * (right - left)
                         missing[bank] -= STEP
                         nc.tensor.matmul_mx(
@@ -168,5 +167,4 @@ def tile_list_heads_silu_kernel(tc, xT, w_words, w_scales, wgt, b, offs, out):
                     nc.scalar.activation(result[:, left:right], sums[bank][:], SILU, bias=bias[:])
                     if right in STORE_ENDS:
                         stored = max(end for end in [0] + STORE_ENDS if end < right)
-                        queue = nc.sync
-                        queue.dma_start(out[:, stored:right], result[:, stored:right])
+                        nc.sync.dma_start(out[:, stored:right], result[:, stored:right])

@@ -22,24 +22,22 @@ E2M1X4 = mybir.dt.float4_e2m1fn_x4
 MULT = mybir.AluOpType.mult
 SILU = mybir.ActivationFunctionType.Silu
 
-EARLY_CALLS = [4, 2]
-LATE_CALLS = [4, 2, 2, 2, 2, 2, 2, 2]
-GATHER_ENDS = [384, 640, 1024]
+CALLS = [4, 4, 4, 4, 2, 2, 2, 2]
+GATHER_ENDS = [384, 1024]
 BANK_ENDS = [384, 640, 768, 896, 1024]
 STORE_ENDS = [640, 1024]
 
 
 def deal_blocks():
-    ahead = sum(EARLY_CALLS) * STEP
-    row = [(0, column) for column in range(0, ahead, STEP)]
-    waiting = [(a, column) for column in range(0, S, STEP) for a in range(LAST) if a > 0 or column >= ahead]
-    for n, width in enumerate(LATE_CALLS):
+    row = []
+    waiting = [(a, column) for column in range(0, S, STEP) for a in range(LAST)]
+    for n, width in enumerate(CALLS):
         row += sorted(waiting[: width - 1]) + [(LAST, n * STEP)]
         waiting = waiting[width - 1 :]
     assert not waiting
     blocks = [(a, column, n * STEP) for n, (a, column) in enumerate(row)]
     calls = []
-    for width in EARLY_CALLS + LATE_CALLS:
+    for width in CALLS:
         calls.append(blocks[:width])
         blocks = blocks[width:]
     return calls

@@ -22,10 +22,10 @@ E2M1X4 = mybir.dt.float4_e2m1fn_x4
 MULT = mybir.AluOpType.mult
 SILU = mybir.ActivationFunctionType.Silu
 
-CALLS = [4, 4, 4, 4, 2, 2, 2, 2]
+CALLS = [4, 2, 4, 2, 4, 2, 4, 2]
 GATHER_ENDS = [384, 1024]
-BANK_ENDS = [384, 640, 768, 896, 1024]
-STORE_ENDS = [640, 1024]
+BANK_ENDS = [512, 640, 768, 896, 1024]
+STORE_ENDS = [768, 1024]
 
 
 def deal_blocks():
@@ -41,16 +41,6 @@ def deal_blocks():
         calls.append(blocks[:width])
         blocks = blocks[width:]
     return calls
-
-
-def runs(blocks):
-    joined = []
-    for a, column, place in blocks:
-        if joined and joined[-1][1] == column and joined[-1][2] + column - joined[-1][0] == place:
-            joined[-1] = (joined[-1][0], column + STEP, joined[-1][2])
-        else:
-            joined.append((column, column + STEP, place))
-    return joined
 
 
 def tile_list_heads_silu_kernel(tc, xT, w_words, w_scales, wgt, b, offs, out):
@@ -126,16 +116,23 @@ def tile_list_heads_silu_kernel(tc, xT, w_words, w_scales, wgt, b, offs, out):
             )
 
         pairs = (slice(0, 2), slice(2, PACK))
+        room = rounded[:].rearrange("p (g n c i) -> p g n c i", n=6, c=STEP, i=PACK)
+        seats = (slice(0, 2), slice(2, 5, 2), slice(3, 6, 2))
         for a in range(PASSES):
-            pieces = [piece for call in calls for piece in runs([block for block in call if block[0] == a])]
             for pair in pairs:
                 gather(a, pair.start, 0, S)
-                ends = GATHER_ENDS if (a, pair) == (LAST, pairs[1]) else [S]
-                for begin, end in zip([0] + ends[:-1], ends):
-                    gather(a, pair.start + 1, begin, end)
-                    for piece in pieces:
-                        if begin <= piece[0] < end:
-                            lay_out(a, *piece, pair)
+                if (a, pair) != (LAST, pairs[1]):
+                    gather(a, pair.start + 1, 0, S)
+                    nc.scalar.copy(
+                        room[:, :, seats[a], :, pair],
+                        picked[a][:, pair, :].rearrange("p i (g n c) -> p g n c i", n=2, c=STEP),
+                    )
+        pieces = [(column, column + STEP, place) for call in calls for a, column, place in call if a == LAST]
+        for begin, end in zip([0] + GATHER_ENDS[:-1], GATHER_ENDS):
+            gather(LAST, PACK - 1, begin, end)
+            for piece in pieces:
+                if begin <= piece[0] < end:
+                    lay_out(LAST, *piece, pairs[1])
 
         missing = [PASSES * (end - begin) for begin, end in banks]
         for call in calls:

@@ -25,7 +25,7 @@ SILU = mybir.ActivationFunctionType.Silu
 CALLS = [4, 2, 4, 2, 4, 2, 4, 2]
 GATHER_ENDS = [384, 1024]
 BANK_ENDS = [512, 640, 768, 896, 1024]
-STORE_ENDS = [768, 1024]
+STORE_ENDS = [512, 768, 1024]
 
 
 def deal_blocks():

@@ -37,9 +37,8 @@ def deal_blocks():
     assert not waiting
     blocks = [(a, column, n * STEP) for n, (a, column) in enumerate(row)]
     calls = []
-    for width in CALLS:
-        calls.append(blocks[:width])
-        blocks = blocks[width:]
+    for first in range(0, len(blocks), 2):
+        calls.append(blocks[first : first + 2])
     return calls
 
 
@@ -62,7 +61,7 @@ def tile_list_heads_silu_kernel(tc, xT, w_words, w_scales, wgt, b, offs, out):
         picked = [held.tile([P, PACK, S], F32, name=f"picked{a}", align_bytes=256) for a in range(PASSES)]
         rounded = held.tile([P, PASSES * S * PACK], BF16, name="rounded", align_bytes=256)
         codes = held.tile([P, PASSES * S], U32, name="codes", align_bytes=256)
-        scales = held.tile([P, PASSES * S], U8, name="scales", align_bytes=256)
+        landing = held.tile([P, 1], F32, name="scales", align_bytes=256)
         result = held.tile([P, S], F32, name="result")
         banks = list(zip([0] + BANK_ENDS[:-1], BANK_ENDS))
         sums = [psum.tile([P, end - begin], F32, name=f"sum{begin}") for begin, end in banks]
@@ -80,13 +79,14 @@ def tile_list_heads_silu_kernel(tc, xT, w_words, w_scales, wgt, b, offs, out):
             nc.sync.dma_start(planes[n][:], by_plane[n // PACK, n % PACK])
             if n == 0:
                 nc.sync.dma_start(lists[:], offs)
+        nc.sync.dma_start(landing[:], b.unsqueeze(1))
+        nc.scalar.copy(bias[:], landing[:])
         nc.sync.dma_start(words[:].bitcast(I32), w_words.bitcast(I32).rearrange("a p n -> p a n"))
         for q in range(4):
             nc.sync.dma_start(
                 wscales[32 * q : 32 * q + 4].bitcast(I32),
                 w_scales.bitcast(I32)[:, 4 * q : 4 * q + 4].rearrange("a r n -> r a n"),
             )
-        nc.sync.dma_start(bias[:], b.unsqueeze(1))
 
         for h in range(2):
             nc.vector.transpose(turned[:, h, :], compact[:, h, :])
@@ -134,6 +134,7 @@ def tile_list_heads_silu_kernel(tc, xT, w_words, w_scales, wgt, b, offs, out):
                 if begin <= piece[0] < end:
                     lay_out(LAST, *piece, pairs[1])
 
+        scales = held.tile([P, PASSES * S], U8, name="scales", align_bytes=256)
         missing = [PASSES * (end - begin) for begin, end in banks]
         for call in calls:
             first, stop = call[0][2], call[-1][2] + STEP

@@ -22,24 +22,10 @@ E2M1X4 = mybir.dt.float4_e2m1fn_x4
 MULT = mybir.AluOpType.mult
 SILU = mybir.ActivationFunctionType.Silu
 
-CALLS = [4, 2, 4, 2, 4, 2, 4, 2]
+CALL = 2
 GATHER_ENDS = [384, 1024]
-BANK_ENDS = [512, 640, 768, 896, 1024]
+BANK_ENDS = [512, 768, 896, 1024]
 STORE_ENDS = [512, 768, 1024]
-
-
-def deal_blocks():
-    row = []
-    waiting = [(a, column) for column in range(0, S, STEP) for a in range(LAST)]
-    for n, width in enumerate(CALLS):
-        row += sorted(waiting[: width - 1]) + [(LAST, n * STEP)]
-        waiting = waiting[width - 1 :]
-    assert not waiting
-    blocks = [(a, column, n * STEP) for n, (a, column) in enumerate(row)]
-    calls = []
-    for first in range(0, len(blocks), 2):
-        calls.append(blocks[first : first + 2])
-    return calls
 
 
 def tile_list_heads_silu_kernel(tc, xT, w_words, w_scales, wgt, b, offs, out):
@@ -48,7 +34,7 @@ def tile_list_heads_silu_kernel(tc, xT, w_words, w_scales, wgt, b, offs, out):
         held = ctx.enter_context(tc.tile_pool(name="held", bufs=1))
         psum = ctx.enter_context(tc.psum_pool(name="psum", bufs=1))
 
-        lists = held.tile([P, S // 16], U16, name="lists")
+        lists = held.tile([P, S // 16], U16, name="lists", align_bytes=256)
         factors = held.tile([P, S], F32, name="factors", align_bytes=256)
         compact = held.tile([P, 2, 32], F32, name="compact", align_bytes=256)
         turned = held.tile([P, 2, 32], F32, name="turned", align_bytes=256)
@@ -62,10 +48,9 @@ def tile_list_heads_silu_kernel(tc, xT, w_words, w_scales, wgt, b, offs, out):
         rounded = held.tile([P, PASSES * S * PACK], BF16, name="rounded", align_bytes=256)
         codes = held.tile([P, PASSES * S], U32, name="codes", align_bytes=256)
         landing = held.tile([P, 1], F32, name="scales", align_bytes=256)
-        result = held.tile([P, S], F32, name="result")
+        result = held.tile([P, S], F32, name="result", align_bytes=256)
         banks = list(zip([0] + BANK_ENDS[:-1], BANK_ENDS))
         sums = [psum.tile([P, end - begin], F32, name=f"sum{begin}") for begin, end in banks]
-        calls = deal_blocks()
 
         by_plane = xT.rearrange("(a p i) t -> a i p t", p=P, i=PACK)
         nc.sync.dma_start(
@@ -108,58 +93,50 @@ def tile_list_heads_silu_kernel(tc, xT, w_words, w_scales, wgt, b, offs, out):
                 MULT,
             )
 
-        def lay_out(a, begin, end, place, pair):
-            room = rounded[:, PACK * place : PACK * (place + end - begin)]
+        room = rounded[:].rearrange("p (n a c i) -> p n a c i", a=PASSES, c=STEP, i=PACK)
+
+        def lay_out(a, pair, begin, end):
             nc.scalar.copy(
-                room.rearrange("p (c i) -> p c i", i=PACK)[:, :, pair],
-                picked[a][:, pair, begin:end].rearrange("p i c -> p c i"),
+                room[:, begin // STEP : end // STEP, a, :, pair],
+                picked[a][:, pair, begin:end].rearrange("p i (n c) -> p n c i", c=STEP),
             )
 
         pairs = (slice(0, 2), slice(2, PACK))
-        room = rounded[:].rearrange("p (g n c i) -> p g n c i", n=6, c=STEP, i=PACK)
-        seats = (slice(0, 2), slice(2, 5, 2), slice(3, 6, 2))
         for a in range(PASSES):
             for pair in pairs:
                 gather(a, pair.start, 0, S)
                 if (a, pair) != (LAST, pairs[1]):
                     gather(a, pair.start + 1, 0, S)
-                    nc.scalar.copy(
-                        room[:, :, seats[a], :, pair],
-                        picked[a][:, pair, :].rearrange("p i (g n c) -> p g n c i", n=2, c=STEP),
-                    )
-        pieces = [(column, column + STEP, place) for call in calls for a, column, place in call if a == LAST]
+                    lay_out(a, pair, 0, S)
         for begin, end in zip([0] + GATHER_ENDS[:-1], GATHER_ENDS):
             gather(LAST, PACK - 1, begin, end)
-            for piece in pieces:
-                if begin <= piece[0] < end:
-                    lay_out(LAST, *piece, pairs[1])
+            for column in range(begin, end, STEP):
+                lay_out(LAST, pairs[1], column, column + STEP)
 
         scales = held.tile([P, PASSES * S], U8, name="scales", align_bytes=256)
-        missing = [PASSES * (end - begin) for begin, end in banks]
-        for call in calls:
-            first, stop = call[0][2], call[-1][2] + STEP
+        for first in range(0, PASSES * S, CALL * STEP):
+            stop = first + CALL * STEP
             nc.vector.quantize_mx(
                 out=codes[:, first:stop].bitcast(E4M3X4),
                 scales=scales[:, first:stop],
                 in_=rounded[:, PACK * first : PACK * stop],
             )
-            for bank, (left, right) in enumerate(banks):
-                was_open = missing[bank] > 0
-                for a, column, place in call:
-                    if left <= column < right:
-                        cols = slice(place, place + STEP)
-                        opens = missing[bank] == PASSES * (right - left)
-                        missing[bank] -= STEP
-                        nc.tensor.matmul_mx(
-                            out=sums[bank][:, column - left : column - left + STEP],
-                            lhsT=words[:, a, :].bitcast(E2M1X4),
-                            lhsT_scale=wscales[:, a, :],
-                            rhs=codes[:, cols].bitcast(E4M3X4),
-                            rhs_scale=scales[:, cols],
-                            start=opens,
-                            stop=missing[bank] == 0,
-                        )
-                if was_open and missing[bank] == 0:
+            for place in range(first, stop, STEP):
+                n, a = divmod(place // STEP, PASSES)
+                column = n * STEP
+                bank = sum(end <= column for end in BANK_ENDS)
+                left, right = banks[bank]
+                closes = a == LAST and column + STEP == right
+                nc.tensor.matmul_mx(
+                    out=sums[bank][:, column - left : column - left + STEP],
+                    lhsT=words[:, a, :].bitcast(E2M1X4),
+                    lhsT_scale=wscales[:, a, :],
+                    rhs=codes[:, place : place + STEP].bitcast(E4M3X4),
+                    rhs_scale=scales[:, place : place + STEP],
+                    start=a == 0 and column == left,
+                    stop=closes,
+                )
+                if closes:
                     nc.scalar.activation(result[:, left:right], sums[bank][:], SILU, bias=bias[:])
                     if right in STORE_ENDS:
                         stored = max(end for end in [0] + STORE_ENDS if end < right)

@@ -22,10 +22,10 @@ E2M1X4 = mybir.dt.float4_e2m1fn_x4
 MULT = mybir.AluOpType.mult
 SILU = mybir.ActivationFunctionType.Silu
 
-CALL = 2
-GATHER_ENDS = [384, 1024]
-BANK_ENDS = [512, 768, 896, 1024]
-STORE_ENDS = [512, 768, 1024]
+CALL = 2 * STEP
+GATHER_ENDS = [384, S]
+BANK_ENDS = [512, 768, 896, S]
+STORE_ENDS = [512, 768, S]
 
 
 def tile_list_heads_silu_kernel(tc, xT, w_words, w_scales, wgt, b, offs, out):
@@ -47,7 +47,7 @@ def tile_list_heads_silu_kernel(tc, xT, w_words, w_scales, wgt, b, offs, out):
         picked = [held.tile([P, PACK, S], F32, name=f"picked{a}", align_bytes=256) for a in range(PASSES)]
         rounded = held.tile([P, PASSES * S * PACK], BF16, name="rounded", align_bytes=256)
         codes = held.tile([P, PASSES * S], U32, name="codes", align_bytes=256)
-        landing = held.tile([P, 1], F32, name="scales", align_bytes=256)
+        landing = held.tile([P, 1], F32, name="landing", tag="landing_then_scales", align_bytes=256)
         result = held.tile([P, S], F32, name="result", align_bytes=256)
         banks = list(zip([0] + BANK_ENDS[:-1], BANK_ENDS))
         sums = [psum.tile([P, end - begin], F32, name=f"sum{begin}") for begin, end in banks]
@@ -113,9 +113,9 @@ def tile_list_heads_silu_kernel(tc, xT, w_words, w_scales, wgt, b, offs, out):
             for column in range(begin, end, STEP):
                 lay_out(LAST, pairs[1], column, column + STEP)
 
-        scales = held.tile([P, PASSES * S], U8, name="scales", align_bytes=256)
-        for first in range(0, PASSES * S, CALL * STEP):
-            stop = first + CALL * STEP
+        scales = held.tile([P, PASSES * S], U8, name="scales", tag="landing_then_scales", align_bytes=256)
+        for first in range(0, PASSES * S, CALL):
+            stop = first + CALL
             nc.vector.quantize_mx(
                 out=codes[:, first:stop].bitcast(E4M3X4),
                 scales=scales[:, first:stop],

@@ -23,7 +23,7 @@ MULT = mybir.AluOpType.mult
 SILU = mybir.ActivationFunctionType.Silu
 
 CALL = 2 * STEP
-GATHER_ENDS = [384, S]
+GATHER_ENDS = [256, S]
 BANK_ENDS = [512, 768, 896, S]
 STORE_ENDS = [512, 768, S]
 
@@ -76,9 +76,9 @@ def tile_list_heads_silu_kernel(tc, xT, w_words, w_scales, wgt, b, offs, out):
         for h in range(2):
             nc.vector.transpose(turned[:, h, :], compact[:, h, :])
         by_block = turned[:].rearrange("p h (g b) -> p b h g", g=2)
-        for half, copy in enumerate((nc.vector.tensor_copy, nc.scalar.copy)):
+        for half in range(2):
             blocks = slice(8 * half, 8 * half + 8)
-            copy(spread[:, blocks], by_block[:, blocks].unsqueeze(4).to_broadcast([P, 8, 2, 2, 16]))
+            nc.vector.tensor_copy(spread[:, blocks], by_block[:, blocks].unsqueeze(4).to_broadcast([P, 8, 2, 2, 16]))
         for half in range(2):
             nc.vector.transpose(
                 factors[:, 512 * half : 512 * half + 512],
@@ -101,21 +101,29 @@ def tile_list_heads_silu_kernel(tc, xT, w_words, w_scales, wgt, b, offs, out):
                 picked[a][:, pair, begin:end].rearrange("p i (n c) -> p n c i", c=STEP),
             )
 
+        def lay_out_whole(a):
+            nc.scalar.copy(
+                room[:, :, a].rearrange("p n (c j) i -> p n c i j", j=4),
+                picked[a][:].rearrange("p i (n c j) -> p n c i j", c=STEP // 4, j=4),
+            )
+
         pairs = (slice(0, 2), slice(2, PACK))
-        for a in range(PASSES):
-            for pair in pairs:
-                gather(a, pair.start, 0, S)
-                if (a, pair) != (LAST, pairs[1]):
-                    gather(a, pair.start + 1, 0, S)
-                    lay_out(a, pair, 0, S)
+        for a in range(LAST):
+            for i in range(PACK):
+                gather(a, i, 0, S)
+            lay_out_whole(a)
+        for i in range(PACK - 1):
+            gather(LAST, i, 0, S)
+            if i == 1:
+                lay_out(LAST, pairs[0], 0, S)
         for begin, end in zip([0] + GATHER_ENDS[:-1], GATHER_ENDS):
             gather(LAST, PACK - 1, begin, end)
             for column in range(begin, end, STEP):
                 lay_out(LAST, pairs[1], column, column + STEP)
 
         scales = held.tile([P, PASSES * S], U8, name="scales", tag="landing_then_scales", align_bytes=256)
-        for first in range(0, PASSES * S, CALL):
-            stop = first + CALL
+        call_ends = list(range(CALL, PASSES * S, CALL)) + [PASSES * S - STEP, PASSES * S]
+        for first, stop in zip([0] + call_ends[:-1], call_ends):
             nc.vector.quantize_mx(
                 out=codes[:, first:stop].bitcast(E4M3X4),
                 scales=scales[:, first:stop],

@@ -8,6 +8,7 @@ PACK = 4
 PASSES = K // (P * PACK)
 LAST = PASSES - 1
 STEP = 128
+ROOMS = 4
 
 FLOPS = 2 * K * M * S
 
@@ -32,14 +33,18 @@ def tile_list_heads_silu_kernel(tc, xT, w_words, w_scales, wgt, b, offs, out):
     nc = tc.nc
     with ExitStack() as ctx:
         held = ctx.enter_context(tc.tile_pool(name="held", bufs=1))
+        rooms = ctx.enter_context(tc.tile_pool(name="rooms", bufs=1))
         psum = ctx.enter_context(tc.psum_pool(name="psum", bufs=1))
+
+        def in_room(n, shape, dtype, name):
+            return rooms.tile(shape, dtype, name=name, align_bytes=256, offset=n % ROOMS * T * 4)
 
         lists = held.tile([P, S // 16], U16, name="lists", align_bytes=256)
         factors = held.tile([P, S], F32, name="factors", align_bytes=256)
-        compact = held.tile([P, 2, 32], F32, name="compact", align_bytes=256)
-        turned = held.tile([P, 2, 32], F32, name="turned", align_bytes=256)
-        spread = held.tile([P, 16, 2, 2, 16], F32, name="spread", align_bytes=256)
-        planes = [held.tile([P, T], F32, name=f"plane{n}", align_bytes=256) for n in range(PASSES * PACK)]
+        compact = in_room(1, [P, 2, 32], F32, "compact")
+        turned = in_room(2, [P, 2, 32], F32, "turned")
+        spread = in_room(3, [P, 16, 2, 2, 16], F32, "spread")
+        planes = [in_room(n, [P, T], F32, f"plane{n}") for n in range(PASSES * PACK)]
         words = held.tile([P, PASSES, 2 * M], U8, name="words", align_bytes=256)
         wscales = held.tile([P, PASSES, M], U8, name="wscales", align_bytes=256)
         bias = held.tile([P, 1], F32, name="bias")
@@ -47,7 +52,7 @@ def tile_list_heads_silu_kernel(tc, xT, w_words, w_scales, wgt, b, offs, out):
         picked = [held.tile([P, PACK, S], F32, name=f"picked{a}", align_bytes=256) for a in range(PASSES)]
         rounded = held.tile([P, PASSES * S * PACK], BF16, name="rounded", align_bytes=256)
         codes = held.tile([P, PASSES * S], U32, name="codes", align_bytes=256)
-        landing = held.tile([P, 1], F32, name="landing", tag="landing_then_scales", align_bytes=256)
+        landing = in_room(9, [P, 1], F32, "landing")
         result = held.tile([P, S], F32, name="result", align_bytes=256)
         banks = list(zip([0] + BANK_ENDS[:-1], BANK_ENDS))
         sums = [psum.tile([P, end - begin], F32, name=f"sum{begin}") for begin, end in banks]
@@ -60,18 +65,12 @@ def tile_list_heads_silu_kernel(tc, xT, w_words, w_scales, wgt, b, offs, out):
         nc.vector.memset(warm[:], 0.0)
         nc.scalar.activation(warm[:], warm[:], SILU)
         nc.vector.memset(wscales[:].rearrange("p a n -> p (a n)").bitcast(I32), 0)
-        for n in range(PASSES * PACK):
+
+        def load(n):
             nc.sync.dma_start(planes[n][:], by_plane[n // PACK, n % PACK])
-            if n == 0:
-                nc.sync.dma_start(lists[:], offs)
-        nc.sync.dma_start(landing[:], b.unsqueeze(1))
-        nc.scalar.copy(bias[:], landing[:])
-        nc.sync.dma_start(words[:].bitcast(I32), w_words.bitcast(I32).rearrange("a p n -> p a n"))
-        for q in range(4):
-            nc.sync.dma_start(
-                wscales[32 * q : 32 * q + 4].bitcast(I32),
-                w_scales.bitcast(I32)[:, 4 * q : 4 * q + 4].rearrange("a r n -> r a n"),
-            )
+
+        load(0)
+        nc.sync.dma_start(lists[:], offs)
 
         for h in range(2):
             nc.vector.transpose(turned[:, h, :], compact[:, h, :])
@@ -85,6 +84,9 @@ def tile_list_heads_silu_kernel(tc, xT, w_words, w_scales, wgt, b, offs, out):
                 spread[:, 8 * half : 8 * half + 8].rearrange("p b h g s -> p (b h g s)"),
             )
 
+        for n in range(1, ROOMS):
+            load(n)
+
         def gather(a, i, begin, end):
             nc.vector.tensor_tensor(
                 picked[a][:, i, begin:end],
@@ -92,6 +94,12 @@ def tile_list_heads_silu_kernel(tc, xT, w_words, w_scales, wgt, b, offs, out):
                 factors[:, begin:end],
                 MULT,
             )
+            n = PACK * a + i
+            if end == S and n + ROOMS < PASSES * PACK:
+                load(n + ROOMS)
+            if n == 9:
+                nc.sync.dma_start(landing[:], b.unsqueeze(1))
+                nc.scalar.copy(bias[:], landing[:])
 
         room = rounded[:].rearrange("p (n a c i) -> p n a c i", a=PASSES, c=STEP, i=PACK)
 
@@ -121,7 +129,13 @@ def tile_list_heads_silu_kernel(tc, xT, w_words, w_scales, wgt, b, offs, out):
             for column in range(begin, end, STEP):
                 lay_out(LAST, pairs[1], column, column + STEP)
 
-        scales = held.tile([P, PASSES * S], U8, name="scales", tag="landing_then_scales", align_bytes=256)
+        nc.sync.dma_start(words[:].bitcast(I32), w_words.bitcast(I32).rearrange("a p n -> p a n"))
+        for q in range(4):
+            nc.sync.dma_start(
+                wscales[32 * q : 32 * q + 4].bitcast(I32),
+                w_scales.bitcast(I32)[:, 4 * q : 4 * q + 4].rearrange("a r n -> r a n"),
+            )
+        scales = in_room(9, [P, PASSES * S], U8, "scales")
         call_ends = list(range(CALL, PASSES * S, CALL)) + [PASSES * S - STEP, PASSES * S]
         for first, stop in zip([0] + call_ends[:-1], call_ends):
             nc.vector.quantize_mx(

@@ -75,13 +75,13 @@ def tile_list_heads_silu_kernel(tc, xT, w_words, w_scales, wgt, b, offs, out):
         for h in range(2):
             nc.vector.transpose(turned[:, h, :], compact[:, h, :])
         by_block = turned[:].rearrange("p h (g b) -> p b h g", g=2)
-        for half in range(2):
-            blocks = slice(8 * half, 8 * half + 8)
-            nc.vector.tensor_copy(spread[:, blocks], by_block[:, blocks].unsqueeze(4).to_broadcast([P, 8, 2, 2, 16]))
-        for half in range(2):
+        for quarter, copy in enumerate((nc.vector.tensor_copy, nc.vector.tensor_copy, nc.scalar.copy, nc.scalar.copy)):
+            blocks = slice(4 * quarter, 4 * quarter + 4)
+            copy(spread[:, blocks], by_block[:, blocks].unsqueeze(4).to_broadcast([P, 4, 2, 2, 16]))
+        for quarter in range(4):
             nc.vector.transpose(
-                factors[:, 512 * half : 512 * half + 512],
-                spread[:, 8 * half : 8 * half + 8].rearrange("p b h g s -> p (b h g s)"),
+                factors[:, 256 * quarter : 256 * quarter + 256],
+                spread[:, 4 * quarter : 4 * quarter + 4].rearrange("p b h g s -> p (b h g s)"),
             )
 
         for n in range(1, ROOMS):

@@ -49,9 +49,9 @@ def tile_list_heads_silu_kernel(tc, xT, w_words, w_scales, wgt, b, offs, out):
         wscales = held.tile([P, PASSES, M], U8, name="wscales", align_bytes=256)
         bias = held.tile([P, 1], F32, name="bias")
         warm = held.tile([P, 1], F32, name="warm")
-        picked = [held.tile([P, PACK, S], F32, name=f"picked{a}", align_bytes=256) for a in range(PASSES)]
+        picked = [held.tile([P, PACK, S + 16], F32, name=f"picked{a}", align_bytes=256)[:, :, 8 : 8 + S] for a in range(PASSES)]
         rounded = held.tile([P, PASSES * S * PACK], BF16, name="rounded", align_bytes=256)
-        codes = held.tile([P, PASSES * S], U32, name="codes", align_bytes=256)
+        codes = held.tile([P, PASSES * S + 32], U32, name="codes", align_bytes=256)[:, 32:]
         landing = in_room(9, [P, 1], F32, "landing")
         result = held.tile([P, S], F32, name="result", align_bytes=256)
         banks = list(zip([0] + BANK_ENDS[:-1], BANK_ENDS))
@@ -112,7 +112,7 @@ def tile_list_heads_silu_kernel(tc, xT, w_words, w_scales, wgt, b, offs, out):
         def lay_out_whole(a):
             nc.scalar.copy(
                 room[:, :, a].rearrange("p n (c j) i -> p n c i j", j=4),
-                picked[a][:].rearrange("p i (n c j) -> p n c i j", c=STEP // 4, j=4),
+                picked[a].rearrange("p i (n c j) -> p n c i j", c=STEP // 4, j=4),
             )
 
         pairs = (slice(0, 2), slice(2, PACK))
@@ -135,7 +135,7 @@ def tile_list_heads_silu_kernel(tc, xT, w_words, w_scales, wgt, b, offs, out):
                 wscales[32 * q : 32 * q + 4].bitcast(I32),
                 w_scales.bitcast(I32)[:, 4 * q : 4 * q + 4].rearrange("a r n -> r a n"),
             )
-        scales = in_room(9, [P, PASSES * S], U8, "scales")
+        scales = in_room(9, [P, PASSES * S + 64], U8, "scales")[:, 64:]
         call_ends = list(range(CALL, PASSES * S, CALL)) + [PASSES * S - STEP, PASSES * S]
         for first, stop in zip([0] + call_ends[:-1], call_ends):
             nc.vector.quantize_mx(

@@ -109,25 +109,28 @@ def tile_list_heads_silu_kernel(tc, xT, w_words, w_scales, wgt, b, offs, out):
                 picked[a][:, pair, begin:end].rearrange("p i (n c) -> p n c i", c=STEP),
             )
 
-        def lay_out_whole(a):
+        def lay_out_whole(a, end):
             nc.scalar.copy(
-                room[:, :, a].rearrange("p n (c j) i -> p n c i j", j=4),
-                picked[a].rearrange("p i (n c j) -> p n c i j", c=STEP // 4, j=4),
+                room[:, : end // STEP, a].rearrange("p n (c j) i -> p n c i j", j=4),
+                picked[a][:, :, :end].rearrange("p i (n c j) -> p n c i j", c=STEP // 4, j=4),
             )
 
         pairs = (slice(0, 2), slice(2, PACK))
         for a in range(LAST):
             for i in range(PACK):
                 gather(a, i, 0, S)
-            lay_out_whole(a)
+            lay_out_whole(a, S)
         for i in range(PACK - 1):
             gather(LAST, i, 0, S)
             if i == 1:
-                lay_out(LAST, pairs[0], 0, S)
+                lay_out(LAST, pairs[0], GATHER_ENDS[0], S)
         for begin, end in zip([0] + GATHER_ENDS[:-1], GATHER_ENDS):
             gather(LAST, PACK - 1, begin, end)
-            for column in range(begin, end, STEP):
-                lay_out(LAST, pairs[1], column, column + STEP)
+            if begin == 0:
+                lay_out_whole(LAST, end)
+            else:
+                for column in range(begin, end, STEP):
+                    lay_out(LAST, pairs[1], column, column + STEP)
 
         nc.sync.dma_start(words[:].bitcast(I32), w_words.bitcast(I32).rearrange("a p n -> p a n"))
         for q in range(4):

@@ -51,7 +51,7 @@ def tile_list_heads_silu_kernel(tc, xT, w_words, w_scales, wgt, b, offs, out):
         warm = held.tile([P, 1], F32, name="warm")
         picked = [held.tile([P, PACK, S + 16], F32, name=f"picked{a}", align_bytes=256)[:, :, 8 : 8 + S] for a in range(PASSES)]
         rounded = held.tile([P, PASSES * S * PACK], BF16, name="rounded", align_bytes=256)
-        codes = held.tile([P, PASSES * S + 32], U32, name="codes", align_bytes=256)[:, 32:]
+        codes = held.tile([P, PASSES * S], U32, name="codes", align_bytes=256)
         landing = in_room(9, [P, 1], F32, "landing")
         result = held.tile([P, S], F32, name="result", align_bytes=256)
         banks = list(zip([0] + BANK_ENDS[:-1], BANK_ENDS))
@@ -75,13 +75,13 @@ def tile_list_heads_silu_kernel(tc, xT, w_words, w_scales, wgt, b, offs, out):
         for h in range(2):
             nc.vector.transpose(turned[:, h, :], compact[:, h, :])
         by_block = turned[:].rearrange("p h (g b) -> p b h g", g=2)
-        for quarter, copy in enumerate((nc.vector.tensor_copy, nc.vector.tensor_copy, nc.scalar.copy, nc.scalar.copy)):
-            blocks = slice(4 * quarter, 4 * quarter + 4)
-            copy(spread[:, blocks], by_block[:, blocks].unsqueeze(4).to_broadcast([P, 4, 2, 2, 16]))
-        for quarter in range(4):
+        for half, copy in enumerate((nc.vector.tensor_copy, nc.scalar.copy)):
+            blocks = slice(8 * half, 8 * half + 8)
+            copy(spread[:, blocks], by_block[:, blocks].unsqueeze(4).to_broadcast([P, 8, 2, 2, 16]))
+        for half in range(2):
             nc.vector.transpose(
-                factors[:, 256 * quarter : 256 * quarter + 256],
-                spread[:, 4 * quarter : 4 * quarter + 4].rearrange("p b h g s -> p (b h g s)"),
+                factors[:, 512 * half : 512 * half + 512],
+                spread[:, 8 * half : 8 * half + 8].rearrange("p b h g s -> p (b h g s)"),
             )
 
         for n in range(1, ROOMS):
@@ -138,7 +138,7 @@ def tile_list_heads_silu_kernel(tc, xT, w_words, w_scales, wgt, b, offs, out):
                 wscales[32 * q : 32 * q + 4].bitcast(I32),
                 w_scales.bitcast(I32)[:, 4 * q : 4 * q + 4].rearrange("a r n -> r a n"),
             )
-        scales = in_room(9, [P, PASSES * S + 64], U8, "scales")[:, 64:]
+        scales = in_room(9, [P, PASSES * S], U8, "scales")
         call_ends = list(range(CALL, PASSES * S, CALL)) + [PASSES * S - STEP, PASSES * S]
         for first, stop in zip([0] + call_ends[:-1], call_ends):
             nc.vector.quantize_mx(

@@ -7,8 +7,8 @@ P = 128
 PACK = 4
 PASSES = K // (P * PACK)
 LAST = PASSES - 1
+PLANES = PASSES * PACK
 STEP = 128
-ROOMS = 4
 
 FLOPS = 2 * K * M * S
 
@@ -23,8 +23,11 @@ E2M1X4 = mybir.dt.float4_e2m1fn_x4
 MULT = mybir.AluOpType.mult
 SILU = mybir.ActivationFunctionType.Silu
 
-CALL = 2 * STEP
-GATHER_ENDS = [256, S]
+ROOMS = 4
+ROW_GAP = 16
+ROW_START = 8
+EARLY = 2 * STEP
+CALL_ENDS = list(range(2 * STEP, PASSES * S, 2 * STEP)) + [PASSES * S - STEP, PASSES * S]
 BANK_ENDS = [512, 768, 896, S]
 STORE_ENDS = [512, 768, S]
 
@@ -44,15 +47,18 @@ def tile_list_heads_silu_kernel(tc, xT, w_words, w_scales, wgt, b, offs, out):
         compact = in_room(1, [P, 2, 32], F32, "compact")
         turned = in_room(2, [P, 2, 32], F32, "turned")
         spread = in_room(3, [P, 16, 2, 2, 16], F32, "spread")
-        planes = [in_room(n, [P, T], F32, f"plane{n}") for n in range(PASSES * PACK)]
+        planes = [in_room(n, [P, T], F32, f"plane{n}") for n in range(PLANES)]
         words = held.tile([P, PASSES, 2 * M], U8, name="words", align_bytes=256)
         wscales = held.tile([P, PASSES, M], U8, name="wscales", align_bytes=256)
         bias = held.tile([P, 1], F32, name="bias")
         warm = held.tile([P, 1], F32, name="warm")
-        picked = [held.tile([P, PACK, S + 16], F32, name=f"picked{a}", align_bytes=256)[:, :, 8 : 8 + S] for a in range(PASSES)]
+        picked = [
+            held.tile([P, PACK, S + ROW_GAP], F32, name=f"picked{a}", align_bytes=256)[:, :, ROW_START : ROW_START + S]
+            for a in range(PASSES)
+        ]
         rounded = held.tile([P, PASSES * S * PACK], BF16, name="rounded", align_bytes=256)
         codes = held.tile([P, PASSES * S], U32, name="codes", align_bytes=256)
-        landing = in_room(9, [P, 1], F32, "landing")
+        landing = in_room(PLANES - 3, [P, 1], F32, "landing")
         result = held.tile([P, S], F32, name="result", align_bytes=256)
         banks = list(zip([0] + BANK_ENDS[:-1], BANK_ENDS))
         sums = [psum.tile([P, end - begin], F32, name=f"sum{begin}") for begin, end in banks]
@@ -87,50 +93,43 @@ def tile_list_heads_silu_kernel(tc, xT, w_words, w_scales, wgt, b, offs, out):
         for n in range(1, ROOMS):
             load(n)
 
-        def gather(a, i, begin, end):
+        def gather(n, begin, end):
             nc.vector.tensor_tensor(
-                picked[a][:, i, begin:end],
-                planes[PACK * a + i][:].indirect(lists[:, begin // 16 : end // 16]),
+                picked[n // PACK][:, n % PACK, begin:end],
+                planes[n][:].indirect(lists[:, begin // 16 : end // 16]),
                 factors[:, begin:end],
                 MULT,
             )
-            n = PACK * a + i
-            if end == S and n + ROOMS < PASSES * PACK:
-                load(n + ROOMS)
-            if n == 9:
-                nc.sync.dma_start(landing[:], b.unsqueeze(1))
-                nc.scalar.copy(bias[:], landing[:])
 
-        room = rounded[:].rearrange("p (n a c i) -> p n a c i", a=PASSES, c=STEP, i=PACK)
-
-        def lay_out(a, pair, begin, end):
-            nc.scalar.copy(
-                room[:, begin // STEP : end // STEP, a, :, pair],
-                picked[a][:, pair, begin:end].rearrange("p i (n c) -> p n c i", c=STEP),
-            )
+        strips = rounded[:].rearrange("p (n a c i) -> p n a c i", a=PASSES, c=STEP, i=PACK)
 
         def lay_out_whole(a, end):
             nc.scalar.copy(
-                room[:, : end // STEP, a].rearrange("p n (c j) i -> p n c i j", j=4),
+                strips[:, : end // STEP, a].rearrange("p n (c j) i -> p n c i j", j=4),
                 picked[a][:, :, :end].rearrange("p i (n c j) -> p n c i j", c=STEP // 4, j=4),
             )
 
-        pairs = (slice(0, 2), slice(2, PACK))
-        for a in range(LAST):
-            for i in range(PACK):
-                gather(a, i, 0, S)
-            lay_out_whole(a, S)
-        for i in range(PACK - 1):
-            gather(LAST, i, 0, S)
-            if i == 1:
-                lay_out(LAST, pairs[0], GATHER_ENDS[0], S)
-        for begin, end in zip([0] + GATHER_ENDS[:-1], GATHER_ENDS):
-            gather(LAST, PACK - 1, begin, end)
-            if begin == 0:
-                lay_out_whole(LAST, end)
-            else:
-                for column in range(begin, end, STEP):
-                    lay_out(LAST, pairs[1], column, column + STEP)
+        def lay_out_pair(pair, begin, end):
+            nc.scalar.copy(
+                strips[:, begin // STEP : end // STEP, LAST, :, pair],
+                picked[LAST][:, pair, begin:end].rearrange("p i (n c) -> p n c i", c=STEP),
+            )
+
+        for n in range(PLANES - 1):
+            gather(n, 0, S)
+            if n + ROOMS < PLANES:
+                load(n + ROOMS)
+            if n % PACK == PACK - 1:
+                lay_out_whole(n // PACK, S)
+            if n == PLANES - 3:
+                nc.sync.dma_start(landing[:], b.unsqueeze(1))
+                nc.scalar.copy(bias[:], landing[:])
+                lay_out_pair(slice(0, 2), EARLY, S)
+        gather(PLANES - 1, 0, EARLY)
+        lay_out_whole(LAST, EARLY)
+        gather(PLANES - 1, EARLY, S)
+        for column in range(EARLY, S, STEP):
+            lay_out_pair(slice(2, PACK), column, column + STEP)
 
         nc.sync.dma_start(words[:].bitcast(I32), w_words.bitcast(I32).rearrange("a p n -> p a n"))
         for q in range(4):
@@ -138,17 +137,17 @@ def tile_list_heads_silu_kernel(tc, xT, w_words, w_scales, wgt, b, offs, out):
                 wscales[32 * q : 32 * q + 4].bitcast(I32),
                 w_scales.bitcast(I32)[:, 4 * q : 4 * q + 4].rearrange("a r n -> r a n"),
             )
-        scales = in_room(9, [P, PASSES * S], U8, "scales")
-        call_ends = list(range(CALL, PASSES * S, CALL)) + [PASSES * S - STEP, PASSES * S]
-        for first, stop in zip([0] + call_ends[:-1], call_ends):
+
+        scales = in_room(PLANES - 3, [P, PASSES * S], U8, "scales")
+        for first, stop in zip([0] + CALL_ENDS[:-1], CALL_ENDS):
             nc.vector.quantize_mx(
                 out=codes[:, first:stop].bitcast(E4M3X4),
                 scales=scales[:, first:stop],
                 in_=rounded[:, PACK * first : PACK * stop],
             )
             for place in range(first, stop, STEP):
-                n, a = divmod(place // STEP, PASSES)
-                column = n * STEP
+                strip, a = divmod(place // STEP, PASSES)
+                column = strip * STEP
                 bank = sum(end <= column for end in BANK_ENDS)
                 left, right = banks[bank]
                 closes = a == LAST and column + STEP == right

@@ -44,12 +44,13 @@ def tile_list_heads_silu_kernel(tc, xT, w_words, w_scales, wgt, b, offs, out):
 
         lists = held.tile([P, S // 16], U16, name="lists", align_bytes=256)
         factors = held.tile([P, S], F32, name="factors", align_bytes=256)
-        compact = in_room(1, [P, 2, 32], F32, "compact")
-        turned = in_room(2, [P, 2, 32], F32, "turned")
-        spread = in_room(3, [P, 16, 2, 2, 16], F32, "spread")
+        rooms_end = ROOMS * T * 4
+        compact = rooms.tile([P, 2, 32], F32, name="compact", align_bytes=256, offset=2 * T * 4 - 256)
+        spread = rooms.tile([P, 16, 2, 2, 16], F32, name="spread", align_bytes=256, offset=rooms_end - 3 * 1024)
+        turned = rooms.tile([P, 2, 32], F32, name="turned", align_bytes=256, offset=rooms_end + 1024)
         planes = [in_room(n, [P, T], F32, f"plane{n}") for n in range(PLANES)]
-        words = held.tile([P, PASSES, 2 * M], U8, name="words", align_bytes=256)
-        wscales = held.tile([P, PASSES, M], U8, name="wscales", align_bytes=256)
+        words = rooms.tile([P, PASSES, 2 * M], U8, name="words", align_bytes=256, offset=rooms_end)
+        wscales = rooms.tile([P, PASSES, M], U8, name="wscales", align_bytes=256, offset=rooms_end + 1024)
         bias = held.tile([P, 1], F32, name="bias")
         warm = held.tile([P, 1], F32, name="warm")
         picked = [
@@ -64,31 +65,32 @@ def tile_list_heads_silu_kernel(tc, xT, w_words, w_scales, wgt, b, offs, out):
         sums = [psum.tile([P, end - begin], F32, name=f"sum{begin}") for begin, end in banks]
 
         by_plane = xT.rearrange("(a p i) t -> a i p t", p=P, i=PACK)
+        nc.scalar.dma_start(planes[0][1:P:2], by_plane[0, 0][1:P:2])
         nc.sync.dma_start(
             compact[:].rearrange("p h r -> p (h r)"),
             wgt.rearrange("(g s) (b r) -> s g b r", s=16, b=16)[0],
         )
         nc.vector.memset(warm[:], 0.0)
         nc.scalar.activation(warm[:], warm[:], SILU)
-        nc.vector.memset(wscales[:].rearrange("p a n -> p (a n)").bitcast(I32), 0)
 
         def load(n):
             nc.sync.dma_start(planes[n][:], by_plane[n // PACK, n % PACK])
 
-        load(0)
         nc.sync.dma_start(lists[:], offs)
+        nc.sync.dma_start(planes[0][0:P:2], by_plane[0, 0][0:P:2])
 
         for h in range(2):
             nc.vector.transpose(turned[:, h, :], compact[:, h, :])
         by_block = turned[:].rearrange("p h (g b) -> p b h g", g=2)
-        for half, copy in enumerate((nc.vector.tensor_copy, nc.scalar.copy)):
-            blocks = slice(8 * half, 8 * half + 8)
-            copy(spread[:, blocks], by_block[:, blocks].unsqueeze(4).to_broadcast([P, 8, 2, 2, 16]))
-        for half in range(2):
+        for quarter, copy in enumerate((nc.vector.tensor_copy,) * 2 + (nc.scalar.copy,) * 2):
+            blocks = slice(4 * quarter, 4 * quarter + 4)
+            copy(spread[:, blocks], by_block[:, blocks].unsqueeze(4).to_broadcast([P, 4, 2, 2, 16]))
+        for quarter in range(4):
             nc.vector.transpose(
-                factors[:, 512 * half : 512 * half + 512],
-                spread[:, 8 * half : 8 * half + 8].rearrange("p b h g s -> p (b h g s)"),
+                factors[:, 256 * quarter : 256 * quarter + 256],
+                spread[:, 4 * quarter : 4 * quarter + 4].rearrange("p b h g s -> p (b h g s)"),
             )
+        nc.vector.memset(wscales[:].rearrange("p a n -> p (a n)").bitcast(I32), 0)
 
         for n in range(1, ROOMS):
             load(n)

@@ -28,6 +28,7 @@ ROW_GAP = 16
 ROW_START = 8
 EARLY = 2 * STEP
 CALL_ENDS = list(range(2 * STEP, PASSES * S, 2 * STEP)) + [PASSES * S - STEP, PASSES * S]
+WIDE_END = 6 * STEP
 BANK_ENDS = [512, 768, 896, S]
 STORE_ENDS = [512, 768, S]
 
@@ -103,19 +104,31 @@ def tile_list_heads_silu_kernel(tc, xT, w_words, w_scales, wgt, b, offs, out):
                 MULT,
             )
 
-        strips = rounded[:].rearrange("p (n a c i) -> p n a c i", a=PASSES, c=STEP, i=PACK)
+        cut = PASSES * WIDE_END * PACK
+        wide = rounded[:, :cut].rearrange("p (n a c i) -> p n a c i", a=PASSES, c=2 * STEP, i=PACK)
+        narrow = rounded[:, cut:].rearrange("p (n a c i) -> p n a c i", a=PASSES, c=STEP, i=PACK)
 
         def lay_out_whole(a, end):
+            wide_end = min(end, WIDE_END)
             nc.scalar.copy(
-                strips[:, : end // STEP, a].rearrange("p n (c j) i -> p n c i j", j=4),
-                picked[a][:, :, :end].rearrange("p i (n c j) -> p n c i j", c=STEP // 4, j=4),
+                wide[:, : wide_end // (2 * STEP), a].rearrange("p n (c j) i -> p n c i j", j=4),
+                picked[a][:, :, :wide_end].rearrange("p i (n c j) -> p n c i j", c=2 * STEP // 4, j=4),
             )
+            if end > WIDE_END:
+                nc.scalar.copy(
+                    narrow[:, :, a].rearrange("p n (c j) i -> p n c i j", j=4),
+                    picked[a][:, :, WIDE_END:].rearrange("p i (n c j) -> p n c i j", c=STEP // 4, j=4),
+                )
 
         def lay_out_pair(pair, begin, end):
-            nc.scalar.copy(
-                strips[:, begin // STEP : end // STEP, LAST, :, pair],
-                picked[LAST][:, pair, begin:end].rearrange("p i (n c) -> p n c i", c=STEP),
-            )
+            if end - begin == STEP and begin < WIDE_END:
+                n, inside = divmod(begin, 2 * STEP)
+                target, width = wide[:, n : n + 1, LAST, inside : inside + STEP, pair], STEP
+            elif begin < WIDE_END:
+                target, width = wide[:, begin // (2 * STEP) : end // (2 * STEP), LAST, :, pair], 2 * STEP
+            else:
+                target, width = narrow[:, (begin - WIDE_END) // STEP : (end - WIDE_END) // STEP, LAST, :, pair], STEP
+            nc.scalar.copy(target, picked[LAST][:, pair, begin:end].rearrange("p i (n c) -> p n c i", c=width))
 
         for n in range(PLANES - 1):
             gather(n, 0, S)
@@ -126,7 +139,8 @@ def tile_list_heads_silu_kernel(tc, xT, w_words, w_scales, wgt, b, offs, out):
             if n == PLANES - 3:
                 nc.sync.dma_start(landing[:], b.unsqueeze(1))
                 nc.scalar.copy(bias[:], landing[:])
-                lay_out_pair(slice(0, 2), EARLY, S)
+                lay_out_pair(slice(0, 2), EARLY, WIDE_END)
+                lay_out_pair(slice(0, 2), WIDE_END, S)
         gather(PLANES - 1, 0, EARLY)
         lay_out_whole(LAST, EARLY)
         gather(PLANES - 1, EARLY, S)
@@ -147,18 +161,19 @@ def tile_list_heads_silu_kernel(tc, xT, w_words, w_scales, wgt, b, offs, out):
                 scales=scales[:, first:stop],
                 in_=rounded[:, PACK * first : PACK * stop],
             )
-            for place in range(first, stop, STEP):
-                strip, a = divmod(place // STEP, PASSES)
-                column = strip * STEP
+            width = 2 * STEP if first < PASSES * WIDE_END else STEP
+            for place in range(first, stop, width):
+                strip, a = divmod(place // width, PASSES)
+                column = strip * width
                 bank = sum(end <= column for end in BANK_ENDS)
                 left, right = banks[bank]
-                closes = a == LAST and column + STEP == right
+                closes = a == LAST and column + width == right
                 nc.tensor.matmul_mx(
-                    out=sums[bank][:, column - left : column - left + STEP],
+                    out=sums[bank][:, column - left : column - left + width],
                     lhsT=words[:, a, :].bitcast(E2M1X4),
                     lhsT_scale=wscales[:, a, :],
-                    rhs=codes[:, place : place + STEP].bitcast(E4M3X4),
-                    rhs_scale=scales[:, place : place + STEP],
+                    rhs=codes[:, place : place + width].bitcast(E4M3X4),
+                    rhs_scale=scales[:, place : place + width],
                     start=a == 0 and column == left,
                     stop=closes,
                 )

@@ -26,11 +26,11 @@ SILU = mybir.ActivationFunctionType.Silu
 ROOMS = 4
 ROW_GAP = 16
 ROW_START = 8
-EARLY = 2 * STEP
-CALL_ENDS = list(range(2 * STEP, PASSES * S, 2 * STEP)) + [PASSES * S - STEP, PASSES * S]
-WIDE_END = 6 * STEP
-BANK_ENDS = [512, 768, 896, S]
-STORE_ENDS = [512, 768, S]
+WIDE_END = 4 * STEP
+STRIP_ENDS = list(range(2 * STEP, WIDE_END, 2 * STEP)) + list(range(WIDE_END, S + 1, STEP))
+EARLY = 3 * STEP
+WHOLE = STRIP_ENDS[0]
+STORE_ENDS = [S - 3 * STEP, S - STEP, S]
 
 
 def tile_list_heads_silu_kernel(tc, xT, w_words, w_scales, wgt, b, offs, out):
@@ -62,8 +62,8 @@ def tile_list_heads_silu_kernel(tc, xT, w_words, w_scales, wgt, b, offs, out):
         codes = held.tile([P, PASSES * S], U32, name="codes", align_bytes=256)
         landing = in_room(PLANES - 3, [P, 1], F32, "landing")
         result = held.tile([P, S], F32, name="result", align_bytes=256)
-        banks = list(zip([0] + BANK_ENDS[:-1], BANK_ENDS))
-        sums = [psum.tile([P, end - begin], F32, name=f"sum{begin}") for begin, end in banks]
+        strips = list(zip([0] + STRIP_ENDS[:-1], STRIP_ENDS))
+        sums = [psum.tile([P, end - begin], F32, name=f"sum{begin}") for begin, end in strips]
 
         by_plane = xT.rearrange("(a p i) t -> a i p t", p=P, i=PACK)
         nc.scalar.dma_start(planes[0][1:P:2], by_plane[0, 0][1:P:2])
@@ -139,13 +139,12 @@ def tile_list_heads_silu_kernel(tc, xT, w_words, w_scales, wgt, b, offs, out):
             if n == PLANES - 3:
                 nc.sync.dma_start(landing[:], b.unsqueeze(1))
                 nc.scalar.copy(bias[:], landing[:])
-                lay_out_pair(slice(0, 2), EARLY, WIDE_END)
+                lay_out_pair(slice(0, 2), WHOLE, WIDE_END)
                 lay_out_pair(slice(0, 2), WIDE_END, S)
         gather(PLANES - 1, 0, EARLY)
-        lay_out_whole(LAST, EARLY)
+        lay_out_whole(LAST, WHOLE)
+        lay_out_pair(slice(2, PACK), WHOLE, EARLY)
         gather(PLANES - 1, EARLY, S)
-        for column in range(EARLY, S, STEP):
-            lay_out_pair(slice(2, PACK), column, column + STEP)
 
         nc.sync.dma_start(words[:].bitcast(I32), w_words.bitcast(I32).rearrange("a p n -> p a n"))
         for q in range(4):
@@ -155,30 +154,47 @@ def tile_list_heads_silu_kernel(tc, xT, w_words, w_scales, wgt, b, offs, out):
             )
 
         scales = in_room(PLANES - 3, [P, PASSES * S], U8, "scales")
-        for first, stop in zip([0] + CALL_ENDS[:-1], CALL_ENDS):
+
+        pieces = [(strip, a) for strip in range(len(strips)) for a in range(PASSES)]
+        wide_pieces = PASSES * WIDE_END // (2 * STEP)
+        calls = [[piece] for piece in pieces[:wide_pieces]]
+        calls[LAST : LAST + 2] = [calls[LAST + 1], calls[LAST]]
+        paired_end = len(pieces) - 2 * PASSES
+        calls.extend(pieces[n : n + 2] for n in range(wide_pieces, paired_end, 2))
+        for n in range(paired_end, len(pieces), PASSES):
+            calls.extend([pieces[n : n + LAST], pieces[n + LAST : n + PASSES]])
+
+        def words_of(strip, a):
+            left, right = strips[strip]
+            first = PASSES * left + a * (right - left)
+            return first, first + right - left
+
+        late = list(range(EARLY, S, STEP))
+        for column in late[:-1]:
+            lay_out_pair(slice(2, PACK), column, column + STEP)
+        for call in calls:
+            first, stop = words_of(*call[0])[0], words_of(*call[-1])[1]
             nc.vector.quantize_mx(
                 out=codes[:, first:stop].bitcast(E4M3X4),
                 scales=scales[:, first:stop],
                 in_=rounded[:, PACK * first : PACK * stop],
             )
-            width = 2 * STEP if first < PASSES * WIDE_END else STEP
-            for place in range(first, stop, width):
-                strip, a = divmod(place // width, PASSES)
-                column = strip * width
-                bank = sum(end <= column for end in BANK_ENDS)
-                left, right = banks[bank]
-                closes = a == LAST and column + width == right
+            for strip, a in call:
+                first, stop = words_of(strip, a)
                 nc.tensor.matmul_mx(
-                    out=sums[bank][:, column - left : column - left + width],
+                    out=sums[strip][:],
                     lhsT=words[:, a, :].bitcast(E2M1X4),
                     lhsT_scale=wscales[:, a, :],
-                    rhs=codes[:, place : place + width].bitcast(E4M3X4),
-                    rhs_scale=scales[:, place : place + width],
-                    start=a == 0 and column == left,
-                    stop=closes,
+                    rhs=codes[:, first:stop].bitcast(E4M3X4),
+                    rhs_scale=scales[:, first:stop],
+                    start=a == 0,
+                    stop=a == LAST,
                 )
-                if closes:
-                    nc.scalar.activation(result[:, left:right], sums[bank][:], SILU, bias=bias[:])
+                if a == LAST:
+                    left, right = strips[strip]
+                    nc.scalar.activation(result[:, left:right], sums[strip][:], SILU, bias=bias[:])
+                    if strip == 0:
+                        lay_out_pair(slice(2, PACK), late[-1], S)
                     if right in STORE_ENDS:
                         stored = max(end for end in [0] + STORE_ENDS if end < right)
                         nc.sync.dma_start(out[:, stored:right], result[:, stored:right])

@@ -24,6 +24,7 @@ MULT = mybir.AluOpType.mult
 SILU = mybir.ActivationFunctionType.Silu
 
 ROOMS = 4
+LEAD = T // 2
 ROW_GAP = 16
 ROW_START = 8
 WIDE_END = 4 * STEP
@@ -40,19 +41,19 @@ def tile_list_heads_silu_kernel(tc, xT, w_words, w_scales, wgt, b, offs, out):
         rooms = ctx.enter_context(tc.tile_pool(name="rooms", bufs=1))
         psum = ctx.enter_context(tc.psum_pool(name="psum", bufs=1))
 
-        def in_room(n, shape, dtype, name):
-            return rooms.tile(shape, dtype, name=name, align_bytes=256, offset=n % ROOMS * T * 4)
-
         lists = held.tile([P, S // 16], U16, name="lists", align_bytes=256)
         factors = held.tile([P, S], F32, name="factors", align_bytes=256)
-        rooms_end = ROOMS * T * 4
+        rooms_end = (ROOMS + 1) * T * 4
         compact = rooms.tile([P, 2, 32], F32, name="compact", align_bytes=256, offset=2 * T * 4 - 256)
         spread = rooms.tile([P, 16, 2, 2, 16], F32, name="spread", align_bytes=256, offset=rooms_end - 3 * 1024)
         turned = rooms.tile([P, 2, 32], F32, name="turned", align_bytes=256, offset=rooms_end + 1024)
-        planes = [in_room(n, [P, T], F32, f"plane{n}") for n in range(PLANES)]
+        starts = [(0, 2, 5, 8)[n % ROOMS] for n in range(PLANES - 2)] + [6, 4]
+        planes = [
+            rooms.tile([P, T], F32, name=f"plane{n}", align_bytes=256, offset=starts[n] * T * 2) for n in range(PLANES)
+        ]
         words = rooms.tile([P, PASSES, 2 * M], U8, name="words", align_bytes=256, offset=rooms_end)
         wscales = rooms.tile([P, PASSES, M], U8, name="wscales", align_bytes=256, offset=rooms_end + 1024)
-        bias = held.tile([P, 1], F32, name="bias")
+        bias = rooms.tile([P, 1], F32, name="bias", align_bytes=256, offset=starts[PLANES - 5] * T * 2)
         warm = held.tile([P, 1], F32, name="warm")
         picked = [
             held.tile([P, PACK, S + ROW_GAP], F32, name=f"picked{a}", align_bytes=256)[:, :, ROW_START : ROW_START + S]
@@ -60,7 +61,6 @@ def tile_list_heads_silu_kernel(tc, xT, w_words, w_scales, wgt, b, offs, out):
         ]
         rounded = held.tile([P, PASSES * S * PACK], BF16, name="rounded", align_bytes=256)
         codes = held.tile([P, PASSES * S], U32, name="codes", align_bytes=256)
-        landing = in_room(PLANES - 3, [P, 1], F32, "landing")
         result = held.tile([P, S], F32, name="result", align_bytes=256)
         strips = list(zip([0] + STRIP_ENDS[:-1], STRIP_ENDS))
         sums = [psum.tile([P, end - begin], F32, name=f"sum{begin}") for begin, end in strips]
@@ -75,7 +75,11 @@ def tile_list_heads_silu_kernel(tc, xT, w_words, w_scales, wgt, b, offs, out):
         nc.scalar.activation(warm[:], warm[:], SILU)
 
         def load(n):
-            nc.sync.dma_start(planes[n][:], by_plane[n // PACK, n % PACK])
+            if n not in range(4, 11):
+                nc.sync.dma_start(planes[n][:], by_plane[n // PACK, n % PACK])
+                return
+            nc.sync.dma_start(planes[n][0:P:2], by_plane[n // PACK, n % PACK][0:P:2])
+            nc.sync.dma_start(planes[n][1:P:2], by_plane[n // PACK, n % PACK][1:P:2])
 
         nc.sync.dma_start(lists[:], offs)
         nc.sync.dma_start(planes[0][0:P:2], by_plane[0, 0][0:P:2])
@@ -132,13 +136,15 @@ def tile_list_heads_silu_kernel(tc, xT, w_words, w_scales, wgt, b, offs, out):
 
         for n in range(PLANES - 1):
             gather(n, 0, S)
-            if n + ROOMS < PLANES:
+            if n + ROOMS < PLANES - 2:
                 load(n + ROOMS)
+            if n + ROOMS == PLANES - 2:
+                nc.sync.dma_start(planes[-1][:, :LEAD], by_plane[LAST, PACK - 1][:, :LEAD])
+                load(n + ROOMS)
+                nc.sync.dma_start(planes[-1][:, LEAD:], by_plane[LAST, PACK - 1][:, LEAD:])
             if n % PACK == PACK - 1:
                 lay_out_whole(n // PACK, S)
             if n == PLANES - 3:
-                nc.sync.dma_start(landing[:], b.unsqueeze(1))
-                nc.scalar.copy(bias[:], landing[:])
                 lay_out_pair(slice(0, 2), WHOLE, WIDE_END)
                 lay_out_pair(slice(0, 2), WIDE_END, S)
         gather(PLANES - 1, 0, EARLY)
@@ -147,13 +153,14 @@ def tile_list_heads_silu_kernel(tc, xT, w_words, w_scales, wgt, b, offs, out):
         gather(PLANES - 1, EARLY, S)
 
         nc.sync.dma_start(words[:].bitcast(I32), w_words.bitcast(I32).rearrange("a p n -> p a n"))
+        nc.sync.dma_start(bias[:], b.unsqueeze(1))
         for q in range(4):
             nc.sync.dma_start(
                 wscales[32 * q : 32 * q + 4].bitcast(I32),
                 w_scales.bitcast(I32)[:, 4 * q : 4 * q + 4].rearrange("a r n -> r a n"),
             )
 
-        scales = in_room(PLANES - 3, [P, PASSES * S], U8, "scales")
+        scales = rooms.tile([P, PASSES * S], U8, name="scales", align_bytes=256, offset=starts[PLANES - 2] * T * 2)
 
         pieces = [(strip, a) for strip in range(len(strips)) for a in range(PASSES)]
         wide_pieces = PASSES * WIDE_END // (2 * STEP)

@@ -79,7 +79,8 @@ def tile_list_heads_silu_kernel(tc, xT, w_words, w_scales, wgt, b, offs, out):
                 nc.sync.dma_start(planes[n][:], by_plane[n // PACK, n % PACK])
                 return
             nc.sync.dma_start(planes[n][0:P:2], by_plane[n // PACK, n % PACK][0:P:2])
-            nc.sync.dma_start(planes[n][1:P:2], by_plane[n // PACK, n % PACK][1:P:2])
+            odd_queue = nc.scalar if n < PLANES - 2 else nc.sync
+            odd_queue.dma_start(planes[n][1:P:2], by_plane[n // PACK, n % PACK][1:P:2])
 
         nc.sync.dma_start(lists[:], offs)
         nc.sync.dma_start(planes[0][0:P:2], by_plane[0, 0][0:P:2])

from contextlib import ExitStack

import concourse.mybir as mybir

K, M, T, S = 1536, 128, 2048, 1024
P = 128
PACK = 4
PASSES = K // (P * PACK)
LAST = PASSES - 1
PLANES = PASSES * PACK
STEP = 128

FLOPS = 2 * K * M * S

F32 = mybir.dt.float32
BF16 = mybir.dt.bfloat16
I32 = mybir.dt.int32
U32 = mybir.dt.uint32
U16 = mybir.dt.uint16
U8 = mybir.dt.uint8
E4M3X4 = mybir.dt.float8_e4m3fn_x4
E2M1X4 = mybir.dt.float4_e2m1fn_x4
MULT = mybir.AluOpType.mult
SILU = mybir.ActivationFunctionType.Silu

ROOMS = 4
LEAD = T // 2
ROW_GAP = 16
ROW_START = 8
WIDE_END = 4 * STEP
STRIP_ENDS = list(range(2 * STEP, WIDE_END, 2 * STEP)) + list(range(WIDE_END, S + 1, STEP))
EARLY = 3 * STEP
WHOLE = STRIP_ENDS[0]
STORE_ENDS = [S - 3 * STEP, S - STEP, S]


def tile_list_heads_silu_kernel(tc, xT, w_words, w_scales, wgt, b, offs, out):
    nc = tc.nc
    with ExitStack() as ctx:
        held = ctx.enter_context(tc.tile_pool(name="held", bufs=1))
        rooms = ctx.enter_context(tc.tile_pool(name="rooms", bufs=1))
        psum = ctx.enter_context(tc.psum_pool(name="psum", bufs=1))

        lists = held.tile([P, S // 16], U16, name="lists", align_bytes=256)
        factors = held.tile([P, S], F32, name="factors", align_bytes=256)
        rooms_end = (ROOMS + 1) * T * 4
        compact = rooms.tile([P, 2, 32], F32, name="compact", align_bytes=256, offset=2 * T * 4 - 256)
        spread = rooms.tile([P, 16, 2, 2, 16], F32, name="spread", align_bytes=256, offset=rooms_end - 3 * 1024)
        turned = rooms.tile([P, 2, 32], F32, name="turned", align_bytes=256, offset=rooms_end + 1024)
        starts = [(0, 2, 5, 8)[n % ROOMS] for n in range(PLANES - 2)] + [6, 4]
        planes = [
            rooms.tile([P, T], F32, name=f"plane{n}", align_bytes=256, offset=starts[n] * T * 2) for n in range(PLANES)
        ]
        words = rooms.tile([P, PASSES, 2 * M], U8, name="words", align_bytes=256, offset=rooms_end)
        wscales = rooms.tile([P, PASSES, M], U8, name="wscales", align_bytes=256, offset=rooms_end + 1024)
        bias = rooms.tile([P, 1], F32, name="bias", align_bytes=256, offset=starts[PLANES - 5] * T * 2)
        warm = held.tile([P, 1], F32, name="warm")
        picked = [
            held.tile([P, PACK, S + ROW_GAP], F32, name=f"picked{a}", align_bytes=256)[:, :, ROW_START : ROW_START + S]
            for a in range(PASSES)
        ]
        rounded = held.tile([P, PASSES * S * PACK], BF16, name="rounded", align_bytes=256)
        codes = held.tile([P, PASSES * S], U32, name="codes", align_bytes=256)
        result = held.tile([P, S], F32, name="result", align_bytes=256)
        strips = list(zip([0] + STRIP_ENDS[:-1], STRIP_ENDS))
        sums = [psum.tile([P, end - begin], F32, name=f"sum{begin}") for begin, end in strips]

        by_plane = xT.rearrange("(a p i) t -> a i p t", p=P, i=PACK)
        nc.scalar.dma_start(planes[0][1:P:2], by_plane[0, 0][1:P:2])
        nc.sync.dma_start(
            compact[:].rearrange("p h r -> p (h r)"),
            wgt.rearrange("(g s) (b r) -> s g b r", s=16, b=16)[0],
        )
        nc.vector.memset(warm[:], 0.0)
        nc.scalar.activation(warm[:], warm[:], SILU)

        def load(n):
            if n not in range(4, 11):
                nc.sync.dma_start(planes[n][:], by_plane[n // PACK, n % PACK])
                return
            nc.sync.dma_start(planes[n][0:P:2], by_plane[n // PACK, n % PACK][0:P:2])
            odd_queue = nc.scalar if n < PLANES - 2 else nc.sync
            odd_queue.dma_start(planes[n][1:P:2], by_plane[n // PACK, n % PACK][1:P:2])

        nc.sync.dma_start(lists[:], offs)
        nc.sync.dma_start(planes[0][0:P:2], by_plane[0, 0][0:P:2])

        for h in range(2):
            nc.vector.transpose(turned[:, h, :], compact[:, h, :])
        by_block = turned[:].rearrange("p h (g b) -> p b h g", g=2)
        for quarter, copy in enumerate((nc.vector.tensor_copy,) * 2 + (nc.scalar.copy,) * 2):
            blocks = slice(4 * quarter, 4 * quarter + 4)
            copy(spread[:, blocks], by_block[:, blocks].unsqueeze(4).to_broadcast([P, 4, 2, 2, 16]))
        for quarter in range(4):
            nc.vector.transpose(
                factors[:, 256 * quarter : 256 * quarter + 256],
                spread[:, 4 * quarter : 4 * quarter + 4].rearrange("p b h g s -> p (b h g s)"),
            )
        nc.vector.memset(wscales[:].rearrange("p a n -> p (a n)").bitcast(I32), 0)

        for n in range(1, ROOMS):
            load(n)

        def gather(n, begin, end):
            nc.vector.tensor_tensor(
                picked[n // PACK][:, n % PACK, begin:end],
                planes[n][:].indirect(lists[:, begin // 16 : end // 16]),
                factors[:, begin:end],
                MULT,
            )

        cut = PASSES * WIDE_END * PACK
        wide = rounded[:, :cut].rearrange("p (n a c i) -> p n a c i", a=PASSES, c=2 * STEP, i=PACK)
        narrow = rounded[:, cut:].rearrange("p (n a c i) -> p n a c i", a=PASSES, c=STEP, i=PACK)

        def lay_out_whole(a, end):
            wide_end = min(end, WIDE_END)
            nc.scalar.copy(
                wide[:, : wide_end // (2 * STEP), a].rearrange("p n (c j) i -> p n c i j", j=4),
                picked[a][:, :, :wide_end].rearrange("p i (n c j) -> p n c i j", c=2 * STEP // 4, j=4),
            )
            if end > WIDE_END:
                nc.scalar.copy(
                    narrow[:, :, a].rearrange("p n (c j) i -> p n c i j", j=4),
                    picked[a][:, :, WIDE_END:].rearrange("p i (n c j) -> p n c i j", c=STEP // 4, j=4),
                )

        def lay_out_pair(pair, begin, end):
            if end - begin == STEP and begin < WIDE_END:
                n, inside = divmod(begin, 2 * STEP)
                target, width = wide[:, n : n + 1, LAST, inside : inside + STEP, pair], STEP
            elif begin < WIDE_END:
                target, width = wide[:, begin // (2 * STEP) : end // (2 * STEP), LAST, :, pair], 2 * STEP
            else:
                target, width = narrow[:, (begin - WIDE_END) // STEP : (end - WIDE_END) // STEP, LAST, :, pair], STEP
            nc.scalar.copy(target, picked[LAST][:, pair, begin:end].rearrange("p i (n c) -> p n c i", c=width))

        for n in range(PLANES - 1):
            gather(n, 0, S)
            if n + ROOMS < PLANES - 2:
                load(n + ROOMS)
            if n + ROOMS == PLANES - 2:
                nc.sync.dma_start(planes[-1][:, :LEAD], by_plane[LAST, PACK - 1][:, :LEAD])
                load(n + ROOMS)
                nc.sync.dma_start(planes[-1][:, LEAD:], by_plane[LAST, PACK - 1][:, LEAD:])
            if n % PACK == PACK - 1:
                lay_out_whole(n // PACK, S)
            if n == PLANES - 3:
                lay_out_pair(slice(0, 2), WHOLE, WIDE_END)
                lay_out_pair(slice(0, 2), WIDE_END, S)
        gather(PLANES - 1, 0, EARLY)
        lay_out_whole(LAST, WHOLE)
        lay_out_pair(slice(2, PACK), WHOLE, EARLY)
        gather(PLANES - 1, EARLY, S)

        nc.sync.dma_start(words[:].bitcast(I32), w_words.bitcast(I32).rearrange("a p n -> p a n"))
        nc.sync.dma_start(bias[:], b.unsqueeze(1))
        for q in range(4):
            nc.sync.dma_start(
                wscales[32 * q : 32 * q + 4].bitcast(I32),
                w_scales.bitcast(I32)[:, 4 * q : 4 * q + 4].rearrange("a r n -> r a n"),
            )

        scales = rooms.tile([P, PASSES * S], U8, name="scales", align_bytes=256, offset=starts[PLANES - 2] * T * 2)

        pieces = [(strip, a) for strip in range(len(strips)) for a in range(PASSES)]
        wide_pieces = PASSES * WIDE_END // (2 * STEP)
        calls = [[piece] for piece in pieces[:wide_pieces]]
        calls[LAST : LAST + 2] = [calls[LAST + 1], calls[LAST]]
        paired_end = len(pieces) - 2 * PASSES
        calls.extend(pieces[n : n + 2] for n in range(wide_pieces, paired_end, 2))
        for n in range(paired_end, len(pieces), PASSES):
            calls.extend([pieces[n : n + LAST], pieces[n + LAST : n + PASSES]])

        def words_of(strip, a):
            left, right = strips[strip]
            first = PASSES * left + a * (right - left)
            return first, first + right - left

        late = list(range(EARLY, S, STEP))
        for column in late[:-1]:
            lay_out_pair(slice(2, PACK), column, column + STEP)
        for call in calls:
            first, stop = words_of(*call[0])[0], words_of(*call[-1])[1]
            nc.vector.quantize_mx(
                out=codes[:, first:stop].bitcast(E4M3X4),
                scales=scales[:, first:stop],
                in_=rounded[:, PACK * first : PACK * stop],
            )
            for strip, a in call:
                first, stop = words_of(strip, a)
                nc.tensor.matmul_mx(
                    out=sums[strip][:],
                    lhsT=words[:, a, :].bitcast(E2M1X4),
                    lhsT_scale=wscales[:, a, :],
                    rhs=codes[:, first:stop].bitcast(E4M3X4),
                    rhs_scale=scales[:, first:stop],
                    start=a == 0,
                    stop=a == LAST,
                )
                if a == LAST:
                    left, right = strips[strip]
                    nc.scalar.activation(result[:, left:right], sums[strip][:], SILU, bias=bias[:])
                    if strip == 0:
                        lay_out_pair(slice(2, PACK), late[-1], S)
                    if right in STORE_ENDS:
                        stored = max(end for end in [0] + STORE_ENDS if end < right)
                        nc.sync.dma_start(out[:, stored:right], result[:, stored:right])
